import numpy as np
import ml_dtypes


def mxq(x, axis, fmt="e4m3"):
    dtype, down = {"e4m3": (ml_dtypes.float8_e4m3fn, 7), "e5m2": (ml_dtypes.float8_e5m2, 14)}[fmt]
    v = np.moveaxis(np.asarray(x, np.float32).astype(ml_dtypes.bfloat16).astype(np.float64), axis, -1)
    blocks = v.reshape(v.shape[:-1] + (-1, 32))
    amax = np.abs(blocks).max(-1, keepdims=True)
    byte = np.maximum(np.where(amax > 0, np.frexp(amax)[1] - 1 + 127, 0) - down, 1)
    scale = np.exp2(byte - 127.0)
    codes = (blocks / scale).astype(np.float32).astype(dtype).astype(np.float64)
    return np.moveaxis((codes * scale).reshape(v.shape), -1, axis)


WIDE = False


def mx_kscale(k):
    if not WIDE:
        return np.ones(k)
    levels = np.array([10, -10, 5, -5, 0])
    if k % 512:
        return np.exp2(np.random.permutation(np.resize(levels, k // 32))).repeat(32)
    a = np.empty((k // 512, 16))
    for p in range(k // 512):
        a[p, :8] = np.random.permutation(np.resize(levels, 8))
        for g in range(8):
            far = levels[np.abs(levels - a[p, g]) >= 10]
            a[p, g + 8] = far[np.random.randint(len(far))]
    return np.exp2(a.ravel()).repeat(32)


def f64(x):
    return np.asarray(x).astype(np.float64)


def striped(idx):
    return np.tile(np.asarray(idx).reshape(-1, 16).T, (8, 1)).astype(np.uint16)


def unstriped(offs):
    return offs[:16].T.reshape(-1).astype(np.int64)


E2M1 = np.array([0.0, 0.5, 1.0, 1.5, 2.0, 3.0, 4.0, 6.0, -0.0, -0.5, -1.0, -1.5, -2.0, -3.0, -4.0, -6.0])


def pack_weight(w, fmt):
    k, n = w.shape
    w = f64(np.asarray(w, np.float32).astype(ml_dtypes.bfloat16)).reshape(k // 32, 32, n)
    amax = np.abs(w).max(1)
    if fmt == "e4m3":
        byte = np.frexp(amax)[1] - 1 + 127 - 7
    else:
        mant, ex = np.frexp(amax / 6.0)
        byte = np.where(mant > 0.5, ex, ex - 1) + 127
    byte = np.clip(np.where(amax > 0, byte, 1), 1, 254)
    scaled = (w * np.exp2(127.0 - byte)[:, None, :]).reshape(k, n).astype(np.float32)
    by_word = np.ascontiguousarray(scaled.reshape(k // 512, 128, 4, n).transpose(0, 1, 3, 2))
    if fmt == "e4m3":
        words = by_word.astype(ml_dtypes.float8_e4m3fn).view(np.uint8)
    else:
        c = by_word.astype(ml_dtypes.float4_e2m1fn).view(np.uint8) & 0xF
        words = (c[..., 0::2] | (c[..., 1::2] << 4)).reshape(k // 512, 128, 2 * n)
    return np.ascontiguousarray(words), np.ascontiguousarray(byte.astype(np.uint8).reshape(k // 512, 16, n))


def unpack_weight(words, scales, fmt):
    g, _, n = scales.shape
    words = np.ascontiguousarray(words).reshape(g, 128, n, -1)
    if fmt == "e4m3":
        vals = words.view(ml_dtypes.float8_e4m3fn).astype(np.float64)
    else:
        nib = np.empty((g, 128, n, 4), np.uint8)
        nib[..., 0::2] = words & 0xF
        nib[..., 1::2] = words >> 4
        vals = E2M1[nib]
    vals = vals * np.repeat(np.exp2(scales.astype(np.float64) - 127.0), 8, axis=1)[..., None]
    return vals.transpose(0, 1, 3, 2).reshape(g * 512, n)


B, N, T, D, NQ = 1, 512, 2048, 512, 512
DV = 512


def sgn(shape):
    return np.random.uniform(0.5, 2.0, shape) * np.where(np.random.standard_normal(shape) < 0, -1.0, 1.0)


def setup_inputs():
    n = np.random.standard_normal
    idx = np.random.permutation(T)[:B * N]
    s = mx_kscale(D)[:, None]
    u = mx_kscale(N)
    ut = np.ones(T)
    ut[idx] = u
    kp = pack_weight(n((D, T)) / s, "e4m3")
    return {
        "qT": (n((B, D, NQ)) * s * (1.00 / np.sqrt(D))).astype(np.float32),
        "k_words": kp[0],
        "k_scales": kp[1],
        "vT": (n((DV, T)) / ut).astype(np.float32),
        "ls": (np.random.uniform(7.0, 7.6, (B, 1, NQ))).astype(np.float32),
        "us": (sgn((B, N, 1)) * u[:, None]).astype(np.float32),
        "offs": striped(idx),
    }


def reference(qT, k_words, k_scales, vT, ls, us, offs):
    idx = unstriped(offs)
    pick = lambda x, which: x[:, which].reshape(x.shape[0], B, -1).transpose(1, 0, 2)
    k = unpack_weight(k_words, k_scales, "e4m3")
    kg = pick(k, idx)
    qq = mxq(f64(qT), 1, "e4m3")
    a = kg.transpose(0, 2, 1) @ qq
    y = np.exp(a - f64(ls)) * f64(us)
    wq = mxq(y, 1, "e4m3")
    o = wq.transpose(0, 2, 1) @ mxq(pick(f64(vT), idx).transpose(0, 2, 1), 1, "e4m3")
    return o

@@ -1,0 +1,173 @@
+from contextlib import ExitStack
+
+import concourse.mybir as mybir
+from concourse.masks import make_identity
+
+F32 = mybir.dt.float32
+BF16 = mybir.dt.bfloat16
+I32 = mybir.dt.int32
+U32 = mybir.dt.uint32
+U16 = mybir.dt.uint16
+U8 = mybir.dt.uint8
+FP8X4 = mybir.dt.float8_e4m3fn_x4
+MULT = mybir.AluOpType.mult
+ADD = mybir.AluOpType.add
+EXP = mybir.ActivationFunctionType.Exp
+
+P = 128
+PACK = 4
+T, N, D, NQ, DV = 2048, 512, 512, 512, 512
+FLOPS = 2 * D * N * NQ + 2 * N * NQ * DV
+
+
+def tile_attend_at_lse_topk_kernel(tc, qT, k_words, k_scales, vT, ls, us, offs, out):
+    nc = tc.nc
+    q_tiles = NQ // P
+    v_blocks = DV // P
+    with ExitStack() as ctx:
+        keep = ctx.enter_context(tc.tile_pool(name="keep", bufs=1))
+        psum = ctx.enter_context(tc.psum_pool(name="psum", bufs=2))
+
+        offsets = keep.tile([P, N // 16], U16, name="offsets")
+        nc.sync.dma_start(offsets[:], offs)
+
+        k_scale_pool = keep.tile([P, T], U8, name="k_scale_pool")
+        nc.vector.memset(k_scale_pool[:].bitcast(I32), 0)
+        for quad in range(4):
+            nc.scalar.dma_start(
+                k_scale_pool[32 * quad : 32 * quad + 4, :].bitcast(I32),
+                k_scales[0, 4 * quad : 4 * quad + 4, :].bitcast(I32),
+            )
+
+        q_raw = keep.tile([P, PACK, NQ], F32, name="q_raw")
+        nc.sync.dma_start(q_raw[:], qT[0].rearrange("(p r) q -> p r q", r=PACK))
+        k_word_pool = keep.tile([P, T], I32, name="k_word_pool")
+        nc.sync.dma_start(k_word_pool[:], k_words[0].rearrange("p t r -> p (t r)").bitcast(I32))
+        v_pool = []
+        for c in range(v_blocks):
+            block = keep.tile([P, T], F32, name="v_pool%d" % c)
+            nc.sync.dma_start(block[:], vT[c * P : (c + 1) * P, :])
+            v_pool.append(block)
+
+        ls_sb = keep.tile([P, q_tiles], F32, name="ls_sb")
+        nc.gpsimd.dma_start(ls_sb[:], ls[0, 0].rearrange("(m j) -> m j", j=q_tiles))
+        us_sb = keep.tile([P, PACK], F32, name="us_sb")
+        nc.gpsimd.dma_start(us_sb[:], us[0].rearrange("(p t) o -> p (t o)", t=PACK))
+        ident = keep.tile([P, P], F32, name="ident")
+        make_identity(nc, ident[:])
+        neg_ls = keep.tile([P, q_tiles], F32, name="neg_ls")
+        nc.gpsimd.tensor_scalar(neg_ls[:], ls_sb[:], -1.0, 0.0, MULT, ADD)
+
+        k_scale = keep.tile([P, N], U8, name="k_scale", align_bytes=64)
+        nc.vector.tensor_copy(k_scale[:], k_scale_pool[:].indirect(offsets[:]))
+
+        q_bf = keep.tile([P, NQ * PACK], BF16, name="q_bf", align_bytes=64)
+        nc.vector.tensor_copy(
+            q_bf[:].rearrange("p (j m r) -> p m r j", j=q_tiles, r=PACK),
+            q_raw[:].rearrange("p r (m j) -> p m r j", j=q_tiles),
+        )
+        k_codes = keep.tile([P, N], U32, name="k_codes", align_bytes=64)
+        q_codes = keep.tile([P, NQ], U32, name="q_codes", align_bytes=64)
+        q_scale = keep.tile([P, NQ], U8, name="q_scale", align_bytes=64)
+        nc.vector.quantize_mx(out=q_codes[:].bitcast(FP8X4), scales=q_scale[:], in_=q_bf[:])
+        nc.vector.tensor_copy(k_codes[:], k_word_pool[:].bitcast(U32).indirect(offsets[:]))
+
+        v_codes = keep.tile([P, DV], U32, name="v_codes", align_bytes=64)
+        v_scale = keep.tile([P, DV], U8, name="v_scale", align_bytes=64)
+        y_codes = keep.tile([P, NQ], U32, name="y_codes", align_bytes=64)
+        y_scale = keep.tile([P, NQ], U8, name="y_scale", align_bytes=64)
+        v_bf = {}
+        y_bf = {}
+
+        def gather_values(c):
+            picked = keep.tile([P, N], BF16, name="v_picked%d" % c)
+            nc.vector.tensor_copy(picked[:], v_pool[c][:].indirect(offsets[:]))
+            words = picked[:].bitcast(F32)
+            turned = psum.tile([P, 2, P], F32, name="v_turned")
+            for u in range(2):
+                nc.tensor.transpose(turned[:, u, :], words[:, u : N // 2 : 2], ident[:])
+            v_bf[c] = keep.tile([P, P * PACK], BF16, name="v_bf%d" % c, align_bytes=64)
+            nc.scalar.copy(
+                v_bf[c][:].bitcast(F32).rearrange("p (e u) -> p e u", u=2),
+                turned[:].rearrange("p u e -> p e u"),
+            )
+
+        def quantize_values(c):
+            cols = slice(c * P, (c + 1) * P)
+            nc.vector.quantize_mx(out=v_codes[:, cols].bitcast(FP8X4), scales=v_scale[:, cols], in_=v_bf[c][:])
+
+        def scores(j):
+            cols = slice(j * P, (j + 1) * P)
+            bank = psum.tile([P, N], F32, name="scores")
+            nc.tensor.matmul_mx(
+                out=bank[:],
+                lhsT=q_codes[:, cols].bitcast(FP8X4),
+                lhsT_scale=q_scale[:, cols],
+                rhs=k_codes[:].bitcast(FP8X4),
+                rhs_scale=k_scale[:],
+                start=True,
+                stop=True,
+            )
+            expd = keep.tile([P, PACK, P], F32, name="expd%d" % j)
+            nc.scalar.activation(
+                expd[:], bank[:].rearrange("m (p t) -> m t p", t=PACK), EXP, bias=neg_ls[:, j : j + 1], scale=1.0
+            )
+            return expd
+
+        def weights(j, expd):
+            turned = psum.tile([P, PACK, P], F32, name="y_turned")
+            for t in range(PACK):
+                nc.tensor.transpose(turned[:, t, :], expd[:, t, :], ident[:])
+            y_bf[j] = keep.tile([P, P * PACK], BF16, name="y_bf%d" % j, align_bytes=64)
+            nc.vector.tensor_tensor(
+                y_bf[j][:].rearrange("p (m t) -> p m t", t=PACK),
+                turned[:].rearrange("p t m -> p m t"),
+                us_sb[:].unsqueeze(1).to_broadcast([P, P, PACK]),
+                MULT,
+            )
+
+        def quantize_weights(j):
+            cols = slice(j * P, (j + 1) * P)
+            nc.vector.quantize_mx(out=y_codes[:, cols].bitcast(FP8X4), scales=y_scale[:, cols], in_=y_bf[j][:])
+
+        out_rows = out[0].rearrange("(m j) e -> m j e", j=q_tiles)
+
+        def product(c):
+            cols = slice(c * P, (c + 1) * P)
+            bank = psum.tile([P, q_tiles, P], F32, name="product")
+            for j in range(q_tiles):
+                q_cols = slice(j * P, (j + 1) * P)
+                nc.tensor.matmul_mx(
+                    out=bank[:, j, :],
+                    lhsT=y_codes[:, q_cols].bitcast(FP8X4),
+                    lhsT_scale=y_scale[:, q_cols],
+                    rhs=v_codes[:, cols].bitcast(FP8X4),
+                    rhs_scale=v_scale[:, cols],
+                    start=True,
+                    stop=True,
+                )
+            result = keep.tile([P, q_tiles, P], F32, name="result%d" % c)
+            nc.scalar.copy(result[:], bank[:])
+            nc.sync.dma_start(out_rows[:, :, cols], result[:])
+
+        expd = [scores(j) for j in range(q_tiles)]
+        gather_values(0)
+        weights(0, expd[0])
+        weights(1, expd[1])
+        quantize_values(0)
+        quantize_weights(0)
+        gather_values(1)
+        weights(2, expd[2])
+        quantize_weights(1)
+        weights(3, expd[3])
+        quantize_values(1)
+        quantize_weights(2)
+        quantize_weights(3)
+        gather_values(2)
+        product(0)
+        product(1)
+        quantize_values(2)
+        gather_values(3)
+        product(2)
+        quantize_values(3)
+        product(3)

@@ -11,12 +11,13 @@ U16 = mybir.dt.uint16
 U8 = mybir.dt.uint8
 FP8X4 = mybir.dt.float8_e4m3fn_x4
 MULT = mybir.AluOpType.mult
-ADD = mybir.AluOpType.add
 EXP = mybir.ActivationFunctionType.Exp
 
 P = 128
 PACK = 4
 T, N, D, NQ, DV = 2048, 512, 512, 512, 512
+V_BYTES = T * 4
+GROUPS = ((0, 2), (2, 1), (3, 1))
 FLOPS = 2 * D * N * NQ + 2 * N * NQ * DV
 
 
@@ -26,37 +27,47 @@ def tile_attend_at_lse_topk_kernel(tc, qT, k_words, k_scales, vT, ls, us, offs, 
     v_blocks = DV // P
     with ExitStack() as ctx:
         keep = ctx.enter_context(tc.tile_pool(name="keep", bufs=1))
+        values = ctx.enter_context(tc.tile_pool(name="values", bufs=1))
         psum = ctx.enter_context(tc.psum_pool(name="psum", bufs=2))
+
+        k_scale_rows = keep.tile([P, T // 4], I32, name="k_scale_rows")
+        for quad in range(4):
+            nc.sync.dma_start(
+                k_scale_rows[32 * quad : 32 * quad + 4, :], k_scales[0, 4 * quad : 4 * quad + 4, :].bitcast(I32)
+            )
+        k_scale_pool = keep.tile([P, T], U8, name="k_scale_pool")
+        nc.vector.memset(k_scale_pool[:].bitcast(I32), 0)
+        for quad in range(4):
+            rows = slice(32 * quad, 32 * quad + 4)
+            nc.vector.tensor_copy(k_scale_pool[rows, :].bitcast(I32), k_scale_rows[rows, :])
 
         offsets = keep.tile([P, N // 16], U16, name="offsets")
         nc.sync.dma_start(offsets[:], offs)
 
-        k_scale_pool = keep.tile([P, T], U8, name="k_scale_pool")
-        nc.vector.memset(k_scale_pool[:].bitcast(I32), 0)
-        for quad in range(4):
-            nc.scalar.dma_start(
-                k_scale_pool[32 * quad : 32 * quad + 4, :].bitcast(I32),
-                k_scales[0, 4 * quad : 4 * quad + 4, :].bitcast(I32),
-            )
-
         q_raw = keep.tile([P, PACK, NQ], F32, name="q_raw")
         nc.sync.dma_start(q_raw[:], qT[0].rearrange("(p r) q -> p r q", r=PACK))
+        us_sb = keep.tile([P, PACK], F32, name="us_sb")
+        nc.sync.dma_start(us_sb[:], us[0].rearrange("(p t) o -> p (t o)", t=PACK))
         k_word_pool = keep.tile([P, T], I32, name="k_word_pool")
         nc.sync.dma_start(k_word_pool[:], k_words[0].rearrange("p t r -> p (t r)").bitcast(I32))
+        ls_sb = keep.tile([P, q_tiles], F32, name="ls_sb")
+        nc.sync.dma_start(ls_sb[:], ls[0, 0].rearrange("(m j) -> m j", j=q_tiles))
         v_pool = []
         for c in range(v_blocks):
-            block = keep.tile([P, T], F32, name="v_pool%d" % c)
+            block = values.tile([P, T], F32, name="v_pool%d" % c, offset=c * V_BYTES)
             nc.sync.dma_start(block[:], vT[c * P : (c + 1) * P, :])
             v_pool.append(block)
 
-        ls_sb = keep.tile([P, q_tiles], F32, name="ls_sb")
-        nc.gpsimd.dma_start(ls_sb[:], ls[0, 0].rearrange("(m j) -> m j", j=q_tiles))
-        us_sb = keep.tile([P, PACK], F32, name="us_sb")
-        nc.gpsimd.dma_start(us_sb[:], us[0].rearrange("(p t) o -> p (t o)", t=PACK))
         ident = keep.tile([P, P], F32, name="ident")
         make_identity(nc, ident[:])
         neg_ls = keep.tile([P, q_tiles], F32, name="neg_ls")
-        nc.gpsimd.tensor_scalar(neg_ls[:], ls_sb[:], -1.0, 0.0, MULT, ADD)
+        nc.vector.tensor_scalar(neg_ls[:], ls_sb[:], -1.0, None, MULT)
+
+        us_rows = psum.tile([P, PACK, P], F32, name="us_rows", bufs=1)
+        for t in range(PACK):
+            nc.tensor.transpose(us_rows[:, t, :], us_sb[:, t : t + 1].to_broadcast([P, P]), ident[:])
+        warm = keep.tile([P, 1], F32, name="warm")
+        nc.scalar.activation(warm[:], ident[:, 0:1], EXP)
 
         k_scale = keep.tile([P, N], U8, name="k_scale", align_bytes=64)
         nc.vector.tensor_copy(k_scale[:], k_scale_pool[:].indirect(offsets[:]))
@@ -72,33 +83,37 @@ def tile_attend_at_lse_topk_kernel(tc, qT, k_words, k_scales, vT, ls, us, offs, 
         nc.vector.quantize_mx(out=q_codes[:].bitcast(FP8X4), scales=q_scale[:], in_=q_bf[:])
         nc.vector.tensor_copy(k_codes[:], k_word_pool[:].bitcast(U32).indirect(offsets[:]))
 
-        v_codes = keep.tile([P, DV], U32, name="v_codes", align_bytes=64)
-        v_scale = keep.tile([P, DV], U8, name="v_scale", align_bytes=64)
-        y_codes = keep.tile([P, NQ], U32, name="y_codes", align_bytes=64)
-        y_scale = keep.tile([P, NQ], U8, name="y_scale", align_bytes=64)
+        v_codes = {}
+        v_scale = {}
         v_bf = {}
-        y_bf = {}
+        y_codes = values.tile([P, NQ], U32, name="y_codes", align_bytes=64, offset=2 * V_BYTES + 1024)
+        y_scale = keep.tile([P, NQ], U8, name="y_scale", align_bytes=64)
+        for first, blocks in GROUPS:
+            v_bf[first] = keep.tile([P, blocks * N], BF16, name="v_bf%d" % first, align_bytes=64)
+        y_bf = keep.tile([P, NQ * PACK], BF16, name="y_bf", align_bytes=64)
 
-        def gather_values(c):
+        def gather_values(c, first):
             picked = keep.tile([P, N], BF16, name="v_picked%d" % c)
             nc.vector.tensor_copy(picked[:], v_pool[c][:].indirect(offsets[:]))
             words = picked[:].bitcast(F32)
-            turned = psum.tile([P, 2, P], F32, name="v_turned")
+            turned = psum.tile([P, 2, P], F32, name="v_turned", tag="turned", bufs=3)
             for u in range(2):
                 nc.tensor.transpose(turned[:, u, :], words[:, u : N // 2 : 2], ident[:])
-            v_bf[c] = keep.tile([P, P * PACK], BF16, name="v_bf%d" % c, align_bytes=64)
             nc.scalar.copy(
-                v_bf[c][:].bitcast(F32).rearrange("p (e u) -> p e u", u=2),
+                v_bf[first][:, (c - first) * N : (c - first + 1) * N].bitcast(F32).rearrange("p (e u) -> p e u", u=2),
                 turned[:].rearrange("p u e -> p e u"),
             )
 
-        def quantize_values(c):
-            cols = slice(c * P, (c + 1) * P)
-            nc.vector.quantize_mx(out=v_codes[:, cols].bitcast(FP8X4), scales=v_scale[:, cols], in_=v_bf[c][:])
+        def quantize_values(first, blocks, offset):
+            v_codes[first] = values.tile(
+                [P, blocks * P], U32, name="v_codes%d" % first, align_bytes=64, offset=offset
+            )
+            v_scale[first] = keep.tile([P, blocks * P], U8, name="v_scale%d" % first, align_bytes=64)
+            nc.vector.quantize_mx(out=v_codes[first][:].bitcast(FP8X4), scales=v_scale[first][:], in_=v_bf[first][:])
 
         def scores(j):
             cols = slice(j * P, (j + 1) * P)
-            bank = psum.tile([P, N], F32, name="scores")
+            bank = psum.tile([P, N], F32, name="scores", tag="mx", bufs=4)
             nc.tensor.matmul_mx(
                 out=bank[:],
                 lhsT=q_codes[:, cols].bitcast(FP8X4),
@@ -108,66 +123,68 @@ def tile_attend_at_lse_topk_kernel(tc, qT, k_words, k_scales, vT, ls, us, offs, 
                 start=True,
                 stop=True,
             )
-            expd = keep.tile([P, PACK, P], F32, name="expd%d" % j)
+            expd = keep.tile([P, 2, P, 2], F32, name="expd%d" % j)
             nc.scalar.activation(
-                expd[:], bank[:].rearrange("m (p t) -> m t p", t=PACK), EXP, bias=neg_ls[:, j : j + 1], scale=1.0
+                expd[:],
+                bank[:].rearrange("m (p u h) -> m u p h", u=2, h=2),
+                EXP,
+                bias=neg_ls[:, j : j + 1],
+                scale=1.0,
             )
             return expd
 
         def weights(j, expd):
-            turned = psum.tile([P, PACK, P], F32, name="y_turned")
-            for t in range(PACK):
-                nc.tensor.transpose(turned[:, t, :], expd[:, t, :], ident[:])
-            y_bf[j] = keep.tile([P, P * PACK], BF16, name="y_bf%d" % j, align_bytes=64)
+            rounded = values.tile([P, N], BF16, name="y_rounded%d" % j, offset=j * N * 2)
             nc.vector.tensor_tensor(
-                y_bf[j][:].rearrange("p (m t) -> p m t", t=PACK),
-                turned[:].rearrange("p t m -> p m t"),
-                us_sb[:].unsqueeze(1).to_broadcast([P, P, PACK]),
+                rounded[:].rearrange("m (u p h) -> m u p h", u=2, h=2),
+                expd[:],
+                us_rows[:].rearrange("m (u h) p -> m u p h", u=2),
                 MULT,
             )
-
-        def quantize_weights(j):
-            cols = slice(j * P, (j + 1) * P)
-            nc.vector.quantize_mx(out=y_codes[:, cols].bitcast(FP8X4), scales=y_scale[:, cols], in_=y_bf[j][:])
+            words = rounded[:].bitcast(F32)
+            turned = psum.tile([P, 2, P], F32, name="y_turned", tag="turned", bufs=3)
+            for u in range(2):
+                nc.tensor.transpose(turned[:, u, :], words[:, u * P : (u + 1) * P], ident[:])
+            nc.scalar.copy(
+                y_bf[:, j * N : (j + 1) * N].bitcast(F32).rearrange("p (m u) -> p m u", u=2),
+                turned[:].rearrange("p u m -> p m u"),
+            )
 
         out_rows = out[0].rearrange("(m j) e -> m j e", j=q_tiles)
 
-        def product(c):
-            cols = slice(c * P, (c + 1) * P)
-            bank = psum.tile([P, q_tiles, P], F32, name="product")
-            for j in range(q_tiles):
-                q_cols = slice(j * P, (j + 1) * P)
-                nc.tensor.matmul_mx(
-                    out=bank[:, j, :],
-                    lhsT=y_codes[:, q_cols].bitcast(FP8X4),
-                    lhsT_scale=y_scale[:, q_cols],
-                    rhs=v_codes[:, cols].bitcast(FP8X4),
-                    rhs_scale=v_scale[:, cols],
-                    start=True,
-                    stop=True,
-                )
-            result = keep.tile([P, q_tiles, P], F32, name="result%d" % c)
-            nc.scalar.copy(result[:], bank[:])
-            nc.sync.dma_start(out_rows[:, :, cols], result[:])
+        def product(first, blocks, tiles_a_bank, engines):
+            width = blocks * P
+            cols = slice(first * P, first * P + width)
+            result = keep.tile([P, q_tiles, width], F32, name="result%d" % first)
+            for half, j0 in enumerate(range(0, q_tiles, tiles_a_bank)):
+                bank = psum.tile([P, tiles_a_bank, width], F32, name="product", tag="mx", bufs=4)
+                for j in range(j0, j0 + tiles_a_bank):
+                    q_cols = slice(j * P, (j + 1) * P)
+                    nc.tensor.matmul_mx(
+                        out=bank[:, j - j0, :],
+                        lhsT=y_codes[:, q_cols].bitcast(FP8X4),
+                        lhsT_scale=y_scale[:, q_cols],
+                        rhs=v_codes[first][:].bitcast(FP8X4),
+                        rhs_scale=v_scale[first][:],
+                        start=True,
+                        stop=True,
+                    )
+                copy, queue = engines[half]
+                copy(result[:, j0 : j0 + tiles_a_bank, :], bank[:])
+                if queue is not None:
+                    queue.dma_start(out_rows[:, j0 : j0 + tiles_a_bank, cols], result[:, j0 : j0 + tiles_a_bank, :])
 
         expd = [scores(j) for j in range(q_tiles)]
-        gather_values(0)
-        weights(0, expd[0])
-        weights(1, expd[1])
-        quantize_values(0)
-        quantize_weights(0)
-        gather_values(1)
-        weights(2, expd[2])
-        quantize_weights(1)
-        weights(3, expd[3])
-        quantize_values(1)
-        quantize_weights(2)
-        quantize_weights(3)
-        gather_values(2)
-        product(0)
-        product(1)
-        quantize_values(2)
-        gather_values(3)
-        product(2)
-        quantize_values(3)
-        product(3)
+        gather_values(0, 0)
+        for j in range(q_tiles):
+            weights(j, expd[j])
+        gather_values(1, 0)
+        gather_values(2, 2)
+        nc.vector.quantize_mx(out=y_codes[:].bitcast(FP8X4), scales=y_scale[:], in_=y_bf[:])
+        quantize_values(0, 2, 2 * V_BYTES)
+        product(0, 2, 2, [(nc.scalar.copy, nc.sync), (nc.scalar.copy, nc.sync)])
+        gather_values(3, 3)
+        quantize_values(2, 1, 3 * V_BYTES)
+        product(2, 1, 4, [(nc.scalar.copy, nc.sync)])
+        quantize_values(3, 1, 3 * V_BYTES + 512)
+        product(3, 1, 2, [(nc.vector.tensor_copy, nc.sync), (nc.scalar.copy, nc.scalar)])

@@ -66,6 +66,8 @@ def tile_attend_at_lse_topk_kernel(tc, qT, k_words, k_scales, vT, ls, us, offs, 
         us_rows = psum.tile([P, PACK, P], F32, name="us_rows", bufs=1)
         for t in range(PACK):
             nc.tensor.transpose(us_rows[:, t, :], us_sb[:, t : t + 1].to_broadcast([P, P]), ident[:])
+        us_rows_sb = keep.tile([P, 2, P, 2], F32, name="us_rows_sb")
+        nc.scalar.copy(us_rows_sb[:], us_rows[:].rearrange("m (u h) p -> m u p h", u=2))
         warm = keep.tile([P, 1], F32, name="warm")
         nc.scalar.activation(warm[:], ident[:, 0:1], EXP)
 
@@ -73,14 +75,20 @@ def tile_attend_at_lse_topk_kernel(tc, qT, k_words, k_scales, vT, ls, us, offs, 
         nc.vector.tensor_copy(k_scale[:], k_scale_pool[:].indirect(offsets[:]))
 
         q_bf = keep.tile([P, NQ * PACK], BF16, name="q_bf", align_bytes=64)
-        nc.vector.tensor_copy(
-            q_bf[:].rearrange("p (j m r) -> p m r j", j=q_tiles, r=PACK),
-            q_raw[:].rearrange("p r (m j) -> p m r j", j=q_tiles),
-        )
+        q_dealt = q_bf[:].rearrange("p (j m r) -> p m r j", j=q_tiles, r=PACK)
+        q_rows = q_raw[:].rearrange("p r (m j) -> p m r j", j=q_tiles)
+        nc.vector.tensor_copy(q_dealt[:, :, :, 0:2], q_rows[:, :, :, 0:2])
+        nc.scalar.copy(q_dealt[:, :, :, 2:4], q_rows[:, :, :, 2:4])
         k_codes = keep.tile([P, N], U32, name="k_codes", align_bytes=64)
         q_codes = keep.tile([P, NQ], U32, name="q_codes", align_bytes=64)
         q_scale = keep.tile([P, NQ], U8, name="q_scale", align_bytes=64)
-        nc.vector.quantize_mx(out=q_codes[:].bitcast(FP8X4), scales=q_scale[:], in_=q_bf[:])
+        for half in range(2):
+            cols = slice(half * 2 * P, (half + 1) * 2 * P)
+            nc.vector.quantize_mx(
+                out=q_codes[:, cols].bitcast(FP8X4),
+                scales=q_scale[:, cols],
+                in_=q_bf[:, half * 2 * N : (half + 1) * 2 * N],
+            )
         nc.vector.tensor_copy(k_codes[:], k_word_pool[:].bitcast(U32).indirect(offsets[:]))
 
         v_codes = {}
@@ -133,21 +141,21 @@ def tile_attend_at_lse_topk_kernel(tc, qT, k_words, k_scales, vT, ls, us, offs, 
             )
             return expd
 
-        def weights(j, expd):
-            rounded = values.tile([P, N], BF16, name="y_rounded%d" % j, offset=j * N * 2)
-            nc.vector.tensor_tensor(
-                rounded[:].rearrange("m (u p h) -> m u p h", u=2, h=2),
-                expd[:],
-                us_rows[:].rearrange("m (u h) p -> m u p h", u=2),
-                MULT,
-            )
-            words = rounded[:].bitcast(F32)
-            turned = psum.tile([P, 2, P], F32, name="y_turned", tag="turned", bufs=3)
-            for u in range(2):
-                nc.tensor.transpose(turned[:, u, :], words[:, u * P : (u + 1) * P], ident[:])
+        def weights(pair, expd):
+            turned = psum.tile([P, 2, 2, P], F32, name="y_turned", tag="turned", bufs=3)
+            for i in range(2):
+                j = 2 * pair + i
+                rounded = values.tile([P, N], BF16, name="y_rounded%d" % j, offset=j * N * 2)
+                engine, factor = (
+                    (nc.gpsimd, us_rows_sb[:]) if j == 0 else (nc.vector, us_rows[:].rearrange("m (u h) p -> m u p h", u=2))
+                )
+                engine.tensor_tensor(rounded[:].rearrange("m (u p h) -> m u p h", u=2, h=2), expd[j][:], factor, MULT)
+                words = rounded[:].bitcast(F32)
+                for u in range(2):
+                    nc.tensor.transpose(turned[:, i, u, :], words[:, u * P : (u + 1) * P], ident[:])
             nc.scalar.copy(
-                y_bf[:, j * N : (j + 1) * N].bitcast(F32).rearrange("p (m u) -> p m u", u=2),
-                turned[:].rearrange("p u m -> p m u"),
+                y_bf[:, 2 * pair * N : 2 * (pair + 1) * N].bitcast(F32).rearrange("p (i m u) -> p i m u", i=2, u=2),
+                turned[:].rearrange("p i u m -> p i m u"),
             )
 
         out_rows = out[0].rearrange("(m j) e -> m j e", j=q_tiles)
@@ -155,7 +163,6 @@ def tile_attend_at_lse_topk_kernel(tc, qT, k_words, k_scales, vT, ls, us, offs, 
         def product(first, blocks, tiles_a_bank, engines):
             width = blocks * P
             cols = slice(first * P, first * P + width)
-            result = keep.tile([P, q_tiles, width], F32, name="result%d" % first)
             for half, j0 in enumerate(range(0, q_tiles, tiles_a_bank)):
                 bank = psum.tile([P, tiles_a_bank, width], F32, name="product", tag="mx", bufs=4)
                 for j in range(j0, j0 + tiles_a_bank):
@@ -169,22 +176,22 @@ def tile_attend_at_lse_topk_kernel(tc, qT, k_words, k_scales, vT, ls, us, offs, 
                         start=True,
                         stop=True,
                     )
-                copy, queue = engines[half]
-                copy(result[:, j0 : j0 + tiles_a_bank, :], bank[:])
-                if queue is not None:
-                    queue.dma_start(out_rows[:, j0 : j0 + tiles_a_bank, cols], result[:, j0 : j0 + tiles_a_bank, :])
+                copy, queue, offset = engines[half]
+                result = values.tile([P, tiles_a_bank, width], F32, name="result%d_%d" % (first, half), offset=offset)
+                copy(result[:], bank[:])
+                queue.dma_start(out_rows[:, j0 : j0 + tiles_a_bank, cols], result[:])
 
         expd = [scores(j) for j in range(q_tiles)]
         gather_values(0, 0)
-        for j in range(q_tiles):
-            weights(j, expd[j])
+        for pair in range(q_tiles // 2):
+            weights(pair, expd)
         gather_values(1, 0)
         gather_values(2, 2)
         nc.vector.quantize_mx(out=y_codes[:].bitcast(FP8X4), scales=y_scale[:], in_=y_bf[:])
         quantize_values(0, 2, 2 * V_BYTES)
-        product(0, 2, 2, [(nc.scalar.copy, nc.sync), (nc.scalar.copy, nc.sync)])
         gather_values(3, 3)
         quantize_values(2, 1, 3 * V_BYTES)
-        product(2, 1, 4, [(nc.scalar.copy, nc.sync)])
+        product(0, 2, 2, [(nc.scalar.copy, nc.sync, V_BYTES), (nc.vector.tensor_copy, nc.sync, 3 * V_BYTES + 2048)])
+        product(2, 1, 4, [(nc.scalar.copy, nc.sync, V_BYTES + 2048)])
         quantize_values(3, 1, 3 * V_BYTES + 512)
-        product(3, 1, 2, [(nc.vector.tensor_copy, nc.sync), (nc.scalar.copy, nc.scalar)])
+        product(3, 1, 2, [(nc.vector.tensor_copy, nc.sync, V_BYTES + 4096), (nc.scalar.copy, nc.scalar, V_BYTES + 6144)])

@@ -30,28 +30,20 @@ def tile_attend_at_lse_topk_kernel(tc, qT, k_words, k_scales, vT, ls, us, offs, 
         values = ctx.enter_context(tc.tile_pool(name="values", bufs=1))
         psum = ctx.enter_context(tc.psum_pool(name="psum", bufs=2))
 
-        k_scale_rows = keep.tile([P, T // 4], I32, name="k_scale_rows")
-        for quad in range(4):
-            nc.sync.dma_start(
-                k_scale_rows[32 * quad : 32 * quad + 4, :], k_scales[0, 4 * quad : 4 * quad + 4, :].bitcast(I32)
-            )
-        k_scale_pool = keep.tile([P, T], U8, name="k_scale_pool")
-        nc.vector.memset(k_scale_pool[:].bitcast(I32), 0)
-        for quad in range(4):
-            rows = slice(32 * quad, 32 * quad + 4)
-            nc.vector.tensor_copy(k_scale_pool[rows, :].bitcast(I32), k_scale_rows[rows, :])
-
         offsets = keep.tile([P, N // 16], U16, name="offsets")
         nc.sync.dma_start(offsets[:], offs)
-
-        q_raw = keep.tile([P, PACK, NQ], F32, name="q_raw")
-        nc.sync.dma_start(q_raw[:], qT[0].rearrange("(p r) q -> p r q", r=PACK))
-        us_sb = keep.tile([P, PACK], F32, name="us_sb")
-        nc.sync.dma_start(us_sb[:], us[0].rearrange("(p t) o -> p (t o)", t=PACK))
         k_word_pool = keep.tile([P, T], I32, name="k_word_pool")
         nc.sync.dma_start(k_word_pool[:], k_words[0].rearrange("p t r -> p (t r)").bitcast(I32))
+        us_sb = keep.tile([P, PACK], F32, name="us_sb")
+        nc.sync.dma_start(us_sb[:], us[0].rearrange("(p t) o -> p (t o)", t=PACK))
         ls_sb = keep.tile([P, q_tiles], F32, name="ls_sb")
         nc.sync.dma_start(ls_sb[:], ls[0, 0].rearrange("(m j) -> m j", j=q_tiles))
+        k_scale_pool = keep.tile([P, T], U8, name="k_scale_pool")
+        nc.vector.memset(k_scale_pool[:].bitcast(I32), 0)
+        for r in range(4):
+            nc.sync.dma_start(k_scale_pool[r:P:32, :].bitcast(I32), k_scales[0, r:16:4, :].bitcast(I32))
+        q_raw = keep.tile([P, PACK, NQ], F32, name="q_raw")
+        nc.sync.dma_start(q_raw[:], qT[0].rearrange("(p r) q -> p r q", r=PACK))
         v_pool = []
         for c in range(v_blocks):
             block = values.tile([P, T], F32, name="v_pool%d" % c, offset=c * V_BYTES)
@@ -71,6 +63,8 @@ def tile_attend_at_lse_topk_kernel(tc, qT, k_words, k_scales, vT, ls, us, offs, 
         warm = keep.tile([P, 1], F32, name="warm")
         nc.scalar.activation(warm[:], ident[:, 0:1], EXP)
 
+        k_codes = keep.tile([P, N], U32, name="k_codes", align_bytes=64)
+        nc.vector.tensor_copy(k_codes[:], k_word_pool[:].bitcast(U32).indirect(offsets[:]))
         k_scale = keep.tile([P, N], U8, name="k_scale", align_bytes=64)
         nc.vector.tensor_copy(k_scale[:], k_scale_pool[:].indirect(offsets[:]))
 
@@ -79,7 +73,6 @@ def tile_attend_at_lse_topk_kernel(tc, qT, k_words, k_scales, vT, ls, us, offs, 
         q_rows = q_raw[:].rearrange("p r (m j) -> p m r j", j=q_tiles)
         nc.vector.tensor_copy(q_dealt[:, :, :, 0:2], q_rows[:, :, :, 0:2])
         nc.scalar.copy(q_dealt[:, :, :, 2:4], q_rows[:, :, :, 2:4])
-        k_codes = keep.tile([P, N], U32, name="k_codes", align_bytes=64)
         q_codes = keep.tile([P, NQ], U32, name="q_codes", align_bytes=64)
         q_scale = keep.tile([P, NQ], U8, name="q_scale", align_bytes=64)
         for half in range(2):
@@ -89,7 +82,6 @@ def tile_attend_at_lse_topk_kernel(tc, qT, k_words, k_scales, vT, ls, us, offs, 
                 scales=q_scale[:, cols],
                 in_=q_bf[:, half * 2 * N : (half + 1) * 2 * N],
             )
-        nc.vector.tensor_copy(k_codes[:], k_word_pool[:].bitcast(U32).indirect(offsets[:]))
 
         v_codes = {}
         v_scale = {}

@@ -11,6 +11,7 @@ U16 = mybir.dt.uint16
 U8 = mybir.dt.uint8
 FP8X4 = mybir.dt.float8_e4m3fn_x4
 MULT = mybir.AluOpType.mult
+COPY = mybir.ActivationFunctionType.Copy
 EXP = mybir.ActivationFunctionType.Exp
 
 P = 128
@@ -53,15 +54,13 @@ def tile_attend_at_lse_topk_kernel(tc, qT, k_words, k_scales, vT, ls, us, offs, 
         ident = keep.tile([P, P], F32, name="ident")
         make_identity(nc, ident[:])
         neg_ls = keep.tile([P, q_tiles], F32, name="neg_ls")
-        nc.vector.tensor_scalar(neg_ls[:], ls_sb[:], -1.0, None, MULT)
+        nc.scalar.activation(neg_ls[:], ls_sb[:], COPY, scale=-1.0)
 
         us_rows = psum.tile([P, PACK, P], F32, name="us_rows", bufs=1)
         for t in range(PACK):
             nc.tensor.transpose(us_rows[:, t, :], us_sb[:, t : t + 1].to_broadcast([P, P]), ident[:])
         us_rows_sb = keep.tile([P, 2, P, 2], F32, name="us_rows_sb")
         nc.scalar.copy(us_rows_sb[:], us_rows[:].rearrange("m (u h) p -> m u p h", u=2))
-        warm = keep.tile([P, 1], F32, name="warm")
-        nc.scalar.activation(warm[:], ident[:, 0:1], EXP)
 
         k_codes = keep.tile([P, N], U32, name="k_codes", align_bytes=64)
         nc.vector.tensor_copy(k_codes[:], k_word_pool[:].bitcast(U32).indirect(offsets[:]))
@@ -183,7 +182,21 @@ def tile_attend_at_lse_topk_kernel(tc, qT, k_words, k_scales, vT, ls, us, offs, 
         quantize_values(0, 2, 2 * V_BYTES)
         gather_values(3, 3)
         quantize_values(2, 1, 3 * V_BYTES)
-        product(0, 2, 2, [(nc.scalar.copy, nc.sync, V_BYTES), (nc.vector.tensor_copy, nc.sync, 3 * V_BYTES + 2048)])
-        product(2, 1, 4, [(nc.scalar.copy, nc.sync, V_BYTES + 2048)])
+        product(0, 2, 2, [(nc.scalar.copy, nc.sync, V_BYTES), (nc.scalar.copy, nc.sync, V_BYTES + 2048)])
+        product(2, 1, 2, [(nc.vector.tensor_copy, nc.sync, 4096), (nc.scalar.copy, nc.sync, 6144)])
         quantize_values(3, 1, 3 * V_BYTES + 512)
-        product(3, 1, 2, [(nc.vector.tensor_copy, nc.sync, V_BYTES + 4096), (nc.scalar.copy, nc.scalar, V_BYTES + 6144)])
+        last = values.tile([P, q_tiles, P], F32, name="last", offset=V_BYTES + 4096)
+        for j in range(q_tiles):
+            bank = psum.tile([P, P], F32, name="last_product", tag=("turned", "mx")[j % 2], bufs=(3, 4)[j % 2])
+            nc.tensor.matmul_mx(
+                out=bank[:],
+                lhsT=y_codes[:, j * P : (j + 1) * P].bitcast(FP8X4),
+                lhsT_scale=y_scale[:, j * P : (j + 1) * P],
+                rhs=v_codes[3][:].bitcast(FP8X4),
+                rhs_scale=v_scale[3][:],
+                start=True,
+                stop=True,
+            )
+            (nc.scalar.copy, nc.vector.tensor_copy)[j % 2](last[:, j, :], bank[:])
+            if j % 2 == 1:
+                (nc.sync, nc.scalar)[j // 2].dma_start(out_rows[:, j - 1 : j + 1, 3 * P :], last[:, j - 1 : j + 1, :])

@@ -85,8 +85,11 @@ def tile_attend_at_lse_topk_kernel(tc, qT, k_words, k_scales, vT, ls, us, offs, 
         v_codes = {}
         v_scale = {}
         v_bf = {}
-        y_codes = values.tile([P, NQ], U32, name="y_codes", align_bytes=64, offset=2 * V_BYTES + 1024)
-        y_scale = keep.tile([P, NQ], U8, name="y_scale", align_bytes=64)
+        y_codes = [
+            values.tile([P, 2 * P], U32, name="y_codes%d" % h, align_bytes=64, offset=2 * V_BYTES + 1024 * (h + 1))
+            for h in range(2)
+        ]
+        y_scale = [keep.tile([P, 2 * P], U8, name="y_scale%d" % h, align_bytes=64) for h in range(2)]
         for first, blocks in GROUPS:
             v_bf[first] = keep.tile([P, blocks * N], BF16, name="v_bf%d" % first, align_bytes=64)
         y_bf = keep.tile([P, NQ * PACK], BF16, name="y_bf", align_bytes=64)
@@ -157,11 +160,11 @@ def tile_attend_at_lse_topk_kernel(tc, qT, k_words, k_scales, vT, ls, us, offs, 
             for half, j0 in enumerate(range(0, q_tiles, tiles_a_bank)):
                 bank = psum.tile([P, tiles_a_bank, width], F32, name="product", tag="mx", bufs=4)
                 for j in range(j0, j0 + tiles_a_bank):
-                    q_cols = slice(j * P, (j + 1) * P)
+                    q_cols = slice((j % 2) * P, (j % 2 + 1) * P)
                     nc.tensor.matmul_mx(
                         out=bank[:, j - j0, :],
-                        lhsT=y_codes[:, q_cols].bitcast(FP8X4),
-                        lhsT_scale=y_scale[:, q_cols],
+                        lhsT=y_codes[j // 2][:, q_cols].bitcast(FP8X4),
+                        lhsT_scale=y_scale[j // 2][:, q_cols],
                         rhs=v_codes[first][:].bitcast(FP8X4),
                         rhs_scale=v_scale[first][:],
                         start=True,
@@ -178,11 +181,15 @@ def tile_attend_at_lse_topk_kernel(tc, qT, k_words, k_scales, vT, ls, us, offs, 
             weights(pair, expd)
         gather_values(1, 0)
         gather_values(2, 2)
-        nc.vector.quantize_mx(out=y_codes[:].bitcast(FP8X4), scales=y_scale[:], in_=y_bf[:])
-        quantize_values(0, 2, 2 * V_BYTES)
+        for h in range(2):
+            nc.vector.quantize_mx(
+                out=y_codes[h][:].bitcast(FP8X4), scales=y_scale[h][:], in_=y_bf[:, 2 * h * N : 2 * (h + 1) * N]
+            )
+            if h == 0:
+                quantize_values(0, 2, 2 * V_BYTES)
         gather_values(3, 3)
         quantize_values(2, 1, 3 * V_BYTES)
-        product(0, 2, 2, [(nc.scalar.copy, nc.sync, V_BYTES), (nc.scalar.copy, nc.sync, V_BYTES + 2048)])
+        product(0, 2, 1, [(nc.scalar.copy, nc.sync, V_BYTES + 1024 * j) for j in range(q_tiles)])
         product(2, 1, 2, [(nc.vector.tensor_copy, nc.sync, 4096), (nc.scalar.copy, nc.sync, 6144)])
         quantize_values(3, 1, 3 * V_BYTES + 512)
         last = values.tile([P, q_tiles, P], F32, name="last", offset=V_BYTES + 4096)
@@ -190,13 +197,12 @@ def tile_attend_at_lse_topk_kernel(tc, qT, k_words, k_scales, vT, ls, us, offs, 
             bank = psum.tile([P, P], F32, name="last_product", tag=("turned", "mx")[j % 2], bufs=(3, 4)[j % 2])
             nc.tensor.matmul_mx(
                 out=bank[:],
-                lhsT=y_codes[:, j * P : (j + 1) * P].bitcast(FP8X4),
-                lhsT_scale=y_scale[:, j * P : (j + 1) * P],
+                lhsT=y_codes[j // 2][:, (j % 2) * P : (j % 2 + 1) * P].bitcast(FP8X4),
+                lhsT_scale=y_scale[j // 2][:, (j % 2) * P : (j % 2 + 1) * P],
                 rhs=v_codes[3][:].bitcast(FP8X4),
                 rhs_scale=v_scale[3][:],
                 start=True,
                 stop=True,
             )
             (nc.scalar.copy, nc.vector.tensor_copy)[j % 2](last[:, j, :], bank[:])
-            if j % 2 == 1:
-                (nc.sync, nc.scalar)[j // 2].dma_start(out_rows[:, j - 1 : j + 1, 3 * P :], last[:, j - 1 : j + 1, :])
+            (nc.scalar, nc.sync)[j % 2].dma_start(out_rows[:, j, 3 * P :], last[:, j, :])

@@ -18,7 +18,6 @@ P = 128
 PACK = 4
 T, N, D, NQ, DV = 2048, 512, 512, 512, 512
 V_BYTES = T * 4
-GROUPS = ((0, 2), (2, 1), (3, 1))
 FLOPS = 2 * D * N * NQ + 2 * N * NQ * DV
 
 
@@ -26,6 +25,7 @@ def tile_attend_at_lse_topk_kernel(tc, qT, k_words, k_scales, vT, ls, us, offs, 
     nc = tc.nc
     q_tiles = NQ // P
     v_blocks = DV // P
+    half = N // 2
     with ExitStack() as ctx:
         keep = ctx.enter_context(tc.tile_pool(name="keep", bufs=1))
         values = ctx.enter_context(tc.tile_pool(name="values", bufs=1))
@@ -33,18 +33,18 @@ def tile_attend_at_lse_topk_kernel(tc, qT, k_words, k_scales, vT, ls, us, offs, 
 
         offsets = keep.tile([P, N // 16], U16, name="offsets")
         nc.sync.dma_start(offsets[:], offs)
-        k_word_pool = keep.tile([P, T], I32, name="k_word_pool")
-        nc.sync.dma_start(k_word_pool[:], k_words[0].rearrange("p t r -> p (t r)").bitcast(I32))
         us_sb = keep.tile([P, PACK], F32, name="us_sb")
         nc.sync.dma_start(us_sb[:], us[0].rearrange("(p t) o -> p (t o)", t=PACK))
         ls_sb = keep.tile([P, q_tiles], F32, name="ls_sb")
         nc.sync.dma_start(ls_sb[:], ls[0, 0].rearrange("(m j) -> m j", j=q_tiles))
-        k_scale_pool = keep.tile([P, T], U8, name="k_scale_pool")
+        q_raw = keep.tile([P, PACK, NQ], F32, name="q_raw")
+        nc.sync.dma_start(q_raw[:], qT[0].rearrange("(p r) q -> p r q", r=PACK))
+        k_scale_pool = values.tile([P, T], U8, name="k_scale_pool", offset=(v_blocks + 1) * V_BYTES)
         nc.vector.memset(k_scale_pool[:].bitcast(I32), 0)
         for r in range(4):
             nc.sync.dma_start(k_scale_pool[r:P:32, :].bitcast(I32), k_scales[0, r:16:4, :].bitcast(I32))
-        q_raw = keep.tile([P, PACK, NQ], F32, name="q_raw")
-        nc.sync.dma_start(q_raw[:], qT[0].rearrange("(p r) q -> p r q", r=PACK))
+        k_word_pool = values.tile([P, T], I32, name="k_word_pool", offset=v_blocks * V_BYTES)
+        nc.sync.dma_start(k_word_pool[:], k_words[0].rearrange("p t r -> p (t r)").bitcast(I32))
         v_pool = []
         for c in range(v_blocks):
             block = values.tile([P, T], F32, name="v_pool%d" % c, offset=c * V_BYTES)
@@ -56,153 +56,165 @@ def tile_attend_at_lse_topk_kernel(tc, qT, k_words, k_scales, vT, ls, us, offs, 
         neg_ls = keep.tile([P, q_tiles], F32, name="neg_ls")
         nc.scalar.activation(neg_ls[:], ls_sb[:], COPY, scale=-1.0)
 
-        us_rows = psum.tile([P, PACK, P], F32, name="us_rows", bufs=1)
+        us_rows = psum.tile([P, PACK, P], F32, name="us_rows", tag="bank0", bufs=1)
         for t in range(PACK):
             nc.tensor.transpose(us_rows[:, t, :], us_sb[:, t : t + 1].to_broadcast([P, P]), ident[:])
+        us_psum = us_rows[:].rearrange("m (u h) p -> m u p h", u=2)
         us_rows_sb = keep.tile([P, 2, P, 2], F32, name="us_rows_sb")
-        nc.scalar.copy(us_rows_sb[:], us_rows[:].rearrange("m (u h) p -> m u p h", u=2))
+        nc.scalar.copy(us_rows_sb[:], us_psum)
 
-        k_codes = keep.tile([P, N], U32, name="k_codes", align_bytes=64)
-        nc.vector.tensor_copy(k_codes[:], k_word_pool[:].bitcast(U32).indirect(offsets[:]))
+        q_rows = q_raw[:].rearrange("p r (m j) -> p m r j", j=q_tiles)
+        q_bf = []
+        for h in range(2):
+            pair = keep.tile([P, 2 * N], BF16, name="q_bf%d" % h, align_bytes=64)
+            nc.scalar.copy(pair[:].rearrange("p (j m r) -> p m r j", j=2, r=PACK), q_rows[:, :, :, 2 * h : 2 * h + 2])
+            q_bf.append(pair)
         k_scale = keep.tile([P, N], U8, name="k_scale", align_bytes=64)
         nc.vector.tensor_copy(k_scale[:], k_scale_pool[:].indirect(offsets[:]))
-
-        q_bf = keep.tile([P, NQ * PACK], BF16, name="q_bf", align_bytes=64)
-        q_dealt = q_bf[:].rearrange("p (j m r) -> p m r j", j=q_tiles, r=PACK)
-        q_rows = q_raw[:].rearrange("p r (m j) -> p m r j", j=q_tiles)
-        nc.vector.tensor_copy(q_dealt[:, :, :, 0:2], q_rows[:, :, :, 0:2])
-        nc.scalar.copy(q_dealt[:, :, :, 2:4], q_rows[:, :, :, 2:4])
-        q_codes = keep.tile([P, NQ], U32, name="q_codes", align_bytes=64)
-        q_scale = keep.tile([P, NQ], U8, name="q_scale", align_bytes=64)
-        for half in range(2):
-            cols = slice(half * 2 * P, (half + 1) * 2 * P)
-            nc.vector.quantize_mx(
-                out=q_codes[:, cols].bitcast(FP8X4),
-                scales=q_scale[:, cols],
-                in_=q_bf[:, half * 2 * N : (half + 1) * 2 * N],
-            )
-
-        v_codes = {}
-        v_scale = {}
-        v_bf = {}
-        y_codes = [
-            values.tile([P, 2 * P], U32, name="y_codes%d" % h, align_bytes=64, offset=2 * V_BYTES + 1024 * (h + 1))
-            for h in range(2)
+        q_codes = [
+            values.tile([P, 2 * P], U32, name="q_codes0", align_bytes=64, offset=(v_blocks + 1) * V_BYTES),
+            values.tile([P, 2 * P], U32, name="q_codes1", align_bytes=64, offset=v_blocks * V_BYTES),
         ]
-        y_scale = [keep.tile([P, 2 * P], U8, name="y_scale%d" % h, align_bytes=64) for h in range(2)]
-        for first, blocks in GROUPS:
-            v_bf[first] = keep.tile([P, blocks * N], BF16, name="v_bf%d" % first, align_bytes=64)
-        y_bf = keep.tile([P, NQ * PACK], BF16, name="y_bf", align_bytes=64)
+        q_scale = [keep.tile([P, 2 * P], U8, name="q_scale%d" % h, align_bytes=64) for h in range(2)]
+        nc.vector.quantize_mx(out=q_codes[0][:].bitcast(FP8X4), scales=q_scale[0][:], in_=q_bf[0][:])
+        k_codes = []
+        for s in range(2):
+            picked_words = keep.tile([P, half], U32, name="k_codes%d" % s, align_bytes=64)
+            nc.vector.tensor_copy(picked_words[:], k_word_pool[:].bitcast(U32).indirect(offsets[:, s * 16 : (s + 1) * 16]))
+            k_codes.append(picked_words)
+        nc.vector.quantize_mx(out=q_codes[1][:].bitcast(FP8X4), scales=q_scale[1][:], in_=q_bf[1][:])
 
-        def gather_values(c, first):
-            picked = keep.tile([P, N], BF16, name="v_picked%d" % c)
-            nc.vector.tensor_copy(picked[:], v_pool[c][:].indirect(offsets[:]))
-            words = picked[:].bitcast(F32)
-            turned = psum.tile([P, 2, P], F32, name="v_turned", tag="turned", bufs=3)
-            for u in range(2):
-                nc.tensor.transpose(turned[:, u, :], words[:, u : N // 2 : 2], ident[:])
-            nc.scalar.copy(
-                v_bf[first][:, (c - first) * N : (c - first + 1) * N].bitcast(F32).rearrange("p (e u) -> p e u", u=2),
-                turned[:].rearrange("p u e -> p e u"),
-            )
+        expd = [keep.tile([P, 2, P, 2], F32, name="expd%d" % j) for j in range(q_tiles)]
 
-        def quantize_values(first, blocks, offset):
-            v_codes[first] = values.tile(
-                [P, blocks * P], U32, name="v_codes%d" % first, align_bytes=64, offset=offset
-            )
-            v_scale[first] = keep.tile([P, blocks * P], U8, name="v_scale%d" % first, align_bytes=64)
-            nc.vector.quantize_mx(out=v_codes[first][:].bitcast(FP8X4), scales=v_scale[first][:], in_=v_bf[first][:])
-
-        def scores(j):
-            cols = slice(j * P, (j + 1) * P)
-            bank = psum.tile([P, N], F32, name="scores", tag="mx", bufs=4)
+        def scores(dest, j, s):
+            cols = slice((j % 2) * P, (j % 2 + 1) * P)
             nc.tensor.matmul_mx(
-                out=bank[:],
-                lhsT=q_codes[:, cols].bitcast(FP8X4),
-                lhsT_scale=q_scale[:, cols],
-                rhs=k_codes[:].bitcast(FP8X4),
-                rhs_scale=k_scale[:],
+                out=dest,
+                lhsT=q_codes[j // 2][:, cols].bitcast(FP8X4),
+                lhsT_scale=q_scale[j // 2][:, cols],
+                rhs=k_codes[s][:].bitcast(FP8X4),
+                rhs_scale=k_scale[:, s * half : (s + 1) * half],
                 start=True,
                 stop=True,
             )
-            expd = keep.tile([P, 2, P, 2], F32, name="expd%d" % j)
-            nc.scalar.activation(
-                expd[:],
-                bank[:].rearrange("m (p u h) -> m u p h", u=2, h=2),
-                EXP,
-                bias=neg_ls[:, j : j + 1],
-                scale=1.0,
-            )
-            return expd
 
-        def weights(pair, expd):
-            turned = psum.tile([P, 2, 2, P], F32, name="y_turned", tag="turned", bufs=3)
-            for i in range(2):
-                j = 2 * pair + i
+        def exponentials(dest, bank, j):
+            nc.scalar.activation(
+                dest, bank.rearrange("m (p u h) -> m u p h", u=2, h=2), EXP, bias=neg_ls[:, j : j + 1], scale=1.0
+            )
+
+        halves = [psum.tile([P, half], F32, name="scores0", tag="bank%d" % (1 + s), bufs=1) for s in range(2)]
+        whole = psum.tile([P, N], F32, name="scores1", tag="bank3", bufs=1)
+        for s in range(2):
+            scores(halves[s][:], 0, s)
+            exponentials(expd[0][:, :, s * P // 2 : (s + 1) * P // 2, :], halves[s][:], 0)
+            scores(whole[:, s * half : (s + 1) * half], 1, s)
+        exponentials(expd[1][:], whole[:], 1)
+        for j in range(2, q_tiles):
+            whole = psum.tile([P, N], F32, name="scores%d" % j, tag="bank%d" % (4, 1)[j - 2], bufs=1)
+            for s in range(2):
+                scores(whole[:, s * half : (s + 1) * half], j, s)
+            exponentials(expd[j][:], whole[:], j)
+
+        y_bf = keep.tile([P, NQ * PACK], BF16, name="y_bf", align_bytes=64)
+        y_codes = values.tile([P, NQ], U32, name="y_codes", align_bytes=64, offset=2 * V_BYTES)
+        y_scale = keep.tile([P, NQ], U8, name="y_scale", align_bytes=64)
+
+        def weights(j):
+            if j < 2:
+                rounded = keep.tile([P, N], BF16, name="y_rounded%d" % j)
+                engine, factor = nc.gpsimd, us_rows_sb[:]
+            else:
                 rounded = values.tile([P, N], BF16, name="y_rounded%d" % j, offset=j * N * 2)
-                engine, factor = (
-                    (nc.gpsimd, us_rows_sb[:]) if j == 0 else (nc.vector, us_rows[:].rearrange("m (u h) p -> m u p h", u=2))
-                )
-                engine.tensor_tensor(rounded[:].rearrange("m (u p h) -> m u p h", u=2, h=2), expd[j][:], factor, MULT)
-                words = rounded[:].bitcast(F32)
-                for u in range(2):
-                    nc.tensor.transpose(turned[:, i, u, :], words[:, u * P : (u + 1) * P], ident[:])
+                engine, factor = nc.vector, us_psum
+            engine.tensor_tensor(rounded[:].rearrange("m (u p h) -> m u p h", u=2, h=2), expd[j][:], factor, MULT)
+            words = rounded[:].bitcast(F32)
+            turned = psum.tile([P, 2, P], F32, name="y_turned", tag="bank%d" % (7, 5, 5, 2)[j], bufs=1)
+            for u in range(2):
+                nc.tensor.transpose(turned[:, u, :], words[:, u * P : (u + 1) * P], ident[:])
             nc.scalar.copy(
-                y_bf[:, 2 * pair * N : 2 * (pair + 1) * N].bitcast(F32).rearrange("p (i m u) -> p i m u", i=2, u=2),
-                turned[:].rearrange("p i u m -> p i m u"),
+                y_bf[:, j * N : (j + 1) * N].bitcast(F32).rearrange("p (m u) -> p m u", u=2),
+                turned[:].rearrange("p u m -> p m u"),
+            )
+
+        v_bf = [
+            keep.tile([P, N], BF16, name="v_bf0", align_bytes=64),
+            values.tile([P, N], BF16, name="v_bf1", align_bytes=64, offset=2 * V_BYTES + 2048),
+            keep.tile([P, N], BF16, name="v_bf2", align_bytes=64),
+            keep.tile([P, N], BF16, name="v_bf3", align_bytes=64),
+        ]
+        picks = []
+
+        def gather_values(c):
+            picked = keep.tile([P, N], BF16, name="v_picked%d" % c)
+            picks.append(picked)
+            nc.vector.tensor_copy(picked[:], v_pool[c][:].indirect(offsets[:]))
+
+        def turn_values(c):
+            words = picks[c][:].bitcast(F32)
+            turned = psum.tile([P, 2, P], F32, name="v_turned", tag="bank%d" % (7, 3, 6, 7)[c], bufs=1)
+            for u in range(2):
+                nc.tensor.transpose(turned[:, u, :], words[:, u : N // 2 : 2], ident[:])
+            nc.scalar.copy(
+                v_bf[c][:].bitcast(F32).rearrange("p (e u) -> p e u", u=2),
+                turned[:].rearrange("p u e -> p e u"),
+            )
+
+        def quantize_values(c, codes, scale):
+            nc.vector.quantize_mx(out=codes.bitcast(FP8X4), scales=scale, in_=v_bf[c][:])
+
+        def multiply(dest, j, codes, scale):
+            cols = slice(j * P, (j + 1) * P)
+            nc.tensor.matmul_mx(
+                out=dest,
+                lhsT=y_codes[:, cols].bitcast(FP8X4),
+                lhsT_scale=y_scale[:, cols],
+                rhs=codes.bitcast(FP8X4),
+                rhs_scale=scale,
+                start=True,
+                stop=True,
             )
 
         out_rows = out[0].rearrange("(m j) e -> m j e", j=q_tiles)
 
-        def product(first, blocks, tiles_a_bank, engines):
-            width = blocks * P
-            cols = slice(first * P, first * P + width)
-            for half, j0 in enumerate(range(0, q_tiles, tiles_a_bank)):
-                bank = psum.tile([P, tiles_a_bank, width], F32, name="product", tag="mx", bufs=4)
-                for j in range(j0, j0 + tiles_a_bank):
-                    q_cols = slice((j % 2) * P, (j % 2 + 1) * P)
-                    nc.tensor.matmul_mx(
-                        out=bank[:, j - j0, :],
-                        lhsT=y_codes[j // 2][:, q_cols].bitcast(FP8X4),
-                        lhsT_scale=y_scale[j // 2][:, q_cols],
-                        rhs=v_codes[first][:].bitcast(FP8X4),
-                        rhs_scale=v_scale[first][:],
-                        start=True,
-                        stop=True,
-                    )
-                copy, queue, offset = engines[half]
-                result = values.tile([P, tiles_a_bank, width], F32, name="result%d_%d" % (first, half), offset=offset)
-                copy(result[:], bank[:])
-                queue.dma_start(out_rows[:, j0 : j0 + tiles_a_bank, cols], result[:])
-
-        expd = [scores(j) for j in range(q_tiles)]
-        gather_values(0, 0)
-        for pair in range(q_tiles // 2):
-            weights(pair, expd)
-        gather_values(1, 0)
-        gather_values(2, 2)
+        gather_values(0)
+        turn_values(0)
+        for j in (0, 2, 3, 1):
+            weights(j)
+        codes = keep.tile([P, 2 * P], U32, name="v_codes01", align_bytes=64)
+        scale = keep.tile([P, 2 * P], U8, name="v_scale01", align_bytes=64)
+        quantize_values(0, codes[:, 0:P], scale[:, 0:P])
+        gather_values(1)
+        gather_values(2)
+        turn_values(1)
+        turn_values(2)
+        nc.vector.quantize_mx(out=y_codes[:].bitcast(FP8X4), scales=y_scale[:], in_=y_bf[:])
+        quantize_values(1, codes[:, P : 2 * P], scale[:, P : 2 * P])
+        for c in range(2):
+            bank = psum.tile([P, q_tiles, P], F32, name="early_product", tag="bank%d" % (4, 1)[c], bufs=1)
+            for j in range(q_tiles):
+                multiply(bank[:, j, :], j, codes[:, c * P : (c + 1) * P], scale[:, c * P : (c + 1) * P])
+            early = keep.tile([P, q_tiles, P], F32, name="early%d" % c)
+            nc.scalar.copy(early[:], bank[:])
+            nc.sync.dma_start(out_rows[:, :, c * P : (c + 1) * P], early[:])
+        gather_values(3)
+        turn_values(3)
+        codes = values.tile([P, P], U32, name="v_codes2", align_bytes=64, offset=3 * V_BYTES)
+        scale = keep.tile([P, P], U8, name="v_scale2", align_bytes=64)
+        quantize_values(2, codes[:], scale[:])
         for h in range(2):
-            nc.vector.quantize_mx(
-                out=y_codes[h][:].bitcast(FP8X4), scales=y_scale[h][:], in_=y_bf[:, 2 * h * N : 2 * (h + 1) * N]
-            )
-            if h == 0:
-                quantize_values(0, 2, 2 * V_BYTES)
-        gather_values(3, 3)
-        quantize_values(2, 1, 3 * V_BYTES)
-        product(0, 2, 1, [(nc.scalar.copy, nc.sync, V_BYTES + 1024 * j) for j in range(q_tiles)])
-        product(2, 1, 2, [(nc.vector.tensor_copy, nc.sync, 4096), (nc.scalar.copy, nc.sync, 6144)])
-        quantize_values(3, 1, 3 * V_BYTES + 512)
-        last = values.tile([P, q_tiles, P], F32, name="last", offset=V_BYTES + 4096)
+            bank = psum.tile([P, 2, P], F32, name="second_product", tag="bank%d" % (5, 0)[h], bufs=1)
+            for i in range(2):
+                multiply(bank[:, i, :], 2 * h + i, codes[:], scale[:])
+            second = keep.tile([P, 2, P], F32, name="second%d" % h)
+            (nc.vector.tensor_copy, nc.scalar.copy)[h](second[:], bank[:])
+            nc.sync.dma_start(out_rows[:, 2 * h : 2 * h + 2, 2 * P : 3 * P], second[:])
+        codes = keep.tile([P, P], U32, name="v_codes3", align_bytes=64)
+        scale = keep.tile([P, P], U8, name="v_scale3", align_bytes=64)
+        quantize_values(3, codes[:], scale[:])
+        last = keep.tile([P, q_tiles, P], F32, name="last")
         for j in range(q_tiles):
-            bank = psum.tile([P, P], F32, name="last_product", tag=("turned", "mx")[j % 2], bufs=(3, 4)[j % 2])
-            nc.tensor.matmul_mx(
-                out=bank[:],
-                lhsT=y_codes[j // 2][:, (j % 2) * P : (j % 2 + 1) * P].bitcast(FP8X4),
-                lhsT_scale=y_scale[j // 2][:, (j % 2) * P : (j % 2 + 1) * P],
-                rhs=v_codes[3][:].bitcast(FP8X4),
-                rhs_scale=v_scale[3][:],
-                start=True,
-                stop=True,
-            )
-            (nc.scalar.copy, nc.vector.tensor_copy)[j % 2](last[:, j, :], bank[:])
-            (nc.scalar, nc.sync)[j % 2].dma_start(out_rows[:, j, 3 * P :], last[:, j, :])
+            bank = psum.tile([P, P], F32, name="last_product", tag="bank%d" % (3, 4, 1, 2)[j], bufs=1)
+            multiply(bank[:], j, codes[:], scale[:])
+            (nc.vector.tensor_copy, nc.scalar.copy)[j % 2](last[:, j, :], bank[:])
+            (nc.sync, nc.scalar)[j % 2].dma_start(out_rows[:, j, 3 * P :], last[:, j, :])

@@ -18,6 +18,7 @@ P = 128
 PACK = 4
 T, N, D, NQ, DV = 2048, 512, 512, 512, 512
 V_BYTES = T * 4
+GROUPS = ((0, 2), (2, 1), (3, 1))
 FLOPS = 2 * D * N * NQ + 2 * N * NQ * DV
 
 
@@ -25,26 +26,25 @@ def tile_attend_at_lse_topk_kernel(tc, qT, k_words, k_scales, vT, ls, us, offs, 
     nc = tc.nc
     q_tiles = NQ // P
     v_blocks = DV // P
-    half = N // 2
     with ExitStack() as ctx:
         keep = ctx.enter_context(tc.tile_pool(name="keep", bufs=1))
         values = ctx.enter_context(tc.tile_pool(name="values", bufs=1))
         psum = ctx.enter_context(tc.psum_pool(name="psum", bufs=2))
 
+        q_raw = keep.tile([P, PACK, NQ], F32, name="q_raw")
+        nc.sync.dma_start(q_raw[:], qT[0].rearrange("(p r) q -> p r q", r=PACK))
         offsets = keep.tile([P, N // 16], U16, name="offsets")
         nc.sync.dma_start(offsets[:], offs)
         us_sb = keep.tile([P, PACK], F32, name="us_sb")
         nc.sync.dma_start(us_sb[:], us[0].rearrange("(p t) o -> p (t o)", t=PACK))
-        ls_sb = keep.tile([P, q_tiles], F32, name="ls_sb")
-        nc.sync.dma_start(ls_sb[:], ls[0, 0].rearrange("(m j) -> m j", j=q_tiles))
-        q_raw = keep.tile([P, PACK, NQ], F32, name="q_raw")
-        nc.sync.dma_start(q_raw[:], qT[0].rearrange("(p r) q -> p r q", r=PACK))
         k_scale_pool = values.tile([P, T], U8, name="k_scale_pool", offset=(v_blocks + 1) * V_BYTES)
         nc.vector.memset(k_scale_pool[:].bitcast(I32), 0)
         for r in range(4):
             nc.sync.dma_start(k_scale_pool[r:P:32, :].bitcast(I32), k_scales[0, r:16:4, :].bitcast(I32))
         k_word_pool = values.tile([P, T], I32, name="k_word_pool", offset=v_blocks * V_BYTES)
         nc.sync.dma_start(k_word_pool[:], k_words[0].rearrange("p t r -> p (t r)").bitcast(I32))
+        ls_sb = keep.tile([P, q_tiles], F32, name="ls_sb")
+        nc.sync.dma_start(ls_sb[:], ls[0, 0].rearrange("(m j) -> m j", j=q_tiles))
         v_pool = []
         for c in range(v_blocks):
             block = values.tile([P, T], F32, name="v_pool%d" % c, offset=c * V_BYTES)
@@ -53,15 +53,12 @@ def tile_attend_at_lse_topk_kernel(tc, qT, k_words, k_scales, vT, ls, us, offs, 
 
         ident = keep.tile([P, P], F32, name="ident")
         make_identity(nc, ident[:])
-        neg_ls = keep.tile([P, q_tiles], F32, name="neg_ls")
-        nc.scalar.activation(neg_ls[:], ls_sb[:], COPY, scale=-1.0)
 
-        us_rows = psum.tile([P, PACK, P], F32, name="us_rows", tag="bank0", bufs=1)
+        us_rows = psum.tile([P, PACK, P], F32, name="us_rows", bufs=1)
         for t in range(PACK):
             nc.tensor.transpose(us_rows[:, t, :], us_sb[:, t : t + 1].to_broadcast([P, P]), ident[:])
-        us_psum = us_rows[:].rearrange("m (u h) p -> m u p h", u=2)
         us_rows_sb = keep.tile([P, 2, P, 2], F32, name="us_rows_sb")
-        nc.scalar.copy(us_rows_sb[:], us_psum)
+        nc.scalar.activation(us_rows_sb[:], us_rows[:].rearrange("m (u h) p -> m u p h", u=2), COPY)
 
         q_rows = q_raw[:].rearrange("p r (m j) -> p m r j", j=q_tiles)
         q_bf = []
@@ -69,6 +66,8 @@ def tile_attend_at_lse_topk_kernel(tc, qT, k_words, k_scales, vT, ls, us, offs, 
             pair = keep.tile([P, 2 * N], BF16, name="q_bf%d" % h, align_bytes=64)
             nc.scalar.copy(pair[:].rearrange("p (j m r) -> p m r j", j=2, r=PACK), q_rows[:, :, :, 2 * h : 2 * h + 2])
             q_bf.append(pair)
+        neg_ls = keep.tile([P, q_tiles], F32, name="neg_ls")
+        nc.scalar.activation(neg_ls[:], ls_sb[:], COPY, scale=-1.0)
         k_scale = keep.tile([P, N], U8, name="k_scale", align_bytes=64)
         nc.vector.tensor_copy(k_scale[:], k_scale_pool[:].indirect(offsets[:]))
         q_codes = [
@@ -79,142 +78,158 @@ def tile_attend_at_lse_topk_kernel(tc, qT, k_words, k_scales, vT, ls, us, offs, 
         nc.vector.quantize_mx(out=q_codes[0][:].bitcast(FP8X4), scales=q_scale[0][:], in_=q_bf[0][:])
         k_codes = []
         for s in range(2):
-            picked_words = keep.tile([P, half], U32, name="k_codes%d" % s, align_bytes=64)
+            picked_words = keep.tile([P, N // 2], U32, name="k_codes%d" % s, align_bytes=64)
             nc.vector.tensor_copy(picked_words[:], k_word_pool[:].bitcast(U32).indirect(offsets[:, s * 16 : (s + 1) * 16]))
             k_codes.append(picked_words)
         nc.vector.quantize_mx(out=q_codes[1][:].bitcast(FP8X4), scales=q_scale[1][:], in_=q_bf[1][:])
 
-        expd = [keep.tile([P, 2, P, 2], F32, name="expd%d" % j) for j in range(q_tiles)]
-
-        def scores(dest, j, s):
-            cols = slice((j % 2) * P, (j % 2 + 1) * P)
-            nc.tensor.matmul_mx(
-                out=dest,
-                lhsT=q_codes[j // 2][:, cols].bitcast(FP8X4),
-                lhsT_scale=q_scale[j // 2][:, cols],
-                rhs=k_codes[s][:].bitcast(FP8X4),
-                rhs_scale=k_scale[:, s * half : (s + 1) * half],
-                start=True,
-                stop=True,
-            )
-
-        def exponentials(dest, bank, j):
-            nc.scalar.activation(
-                dest, bank.rearrange("m (p u h) -> m u p h", u=2, h=2), EXP, bias=neg_ls[:, j : j + 1], scale=1.0
-            )
-
-        halves = [psum.tile([P, half], F32, name="scores0", tag="bank%d" % (1 + s), bufs=1) for s in range(2)]
-        whole = psum.tile([P, N], F32, name="scores1", tag="bank3", bufs=1)
-        for s in range(2):
-            scores(halves[s][:], 0, s)
-            exponentials(expd[0][:, :, s * P // 2 : (s + 1) * P // 2, :], halves[s][:], 0)
-            scores(whole[:, s * half : (s + 1) * half], 1, s)
-        exponentials(expd[1][:], whole[:], 1)
-        for j in range(2, q_tiles):
-            whole = psum.tile([P, N], F32, name="scores%d" % j, tag="bank%d" % (4, 1)[j - 2], bufs=1)
-            for s in range(2):
-                scores(whole[:, s * half : (s + 1) * half], j, s)
-            exponentials(expd[j][:], whole[:], j)
-
-        y_bf = keep.tile([P, NQ * PACK], BF16, name="y_bf", align_bytes=64)
         y_codes = values.tile([P, NQ], U32, name="y_codes", align_bytes=64, offset=2 * V_BYTES)
         y_scale = keep.tile([P, NQ], U8, name="y_scale", align_bytes=64)
-
-        def weights(j):
-            if j < 2:
-                rounded = keep.tile([P, N], BF16, name="y_rounded%d" % j)
-                engine, factor = nc.gpsimd, us_rows_sb[:]
-            else:
-                rounded = values.tile([P, N], BF16, name="y_rounded%d" % j, offset=j * N * 2)
-                engine, factor = nc.vector, us_psum
-            engine.tensor_tensor(rounded[:].rearrange("m (u p h) -> m u p h", u=2, h=2), expd[j][:], factor, MULT)
-            words = rounded[:].bitcast(F32)
-            turned = psum.tile([P, 2, P], F32, name="y_turned", tag="bank%d" % (7, 5, 5, 2)[j], bufs=1)
-            for u in range(2):
-                nc.tensor.transpose(turned[:, u, :], words[:, u * P : (u + 1) * P], ident[:])
-            nc.scalar.copy(
-                y_bf[:, j * N : (j + 1) * N].bitcast(F32).rearrange("p (m u) -> p m u", u=2),
-                turned[:].rearrange("p u m -> p m u"),
-            )
-
+        y_bf = keep.tile([P, NQ * PACK], BF16, name="y_bf", align_bytes=64)
         v_bf = [
             keep.tile([P, N], BF16, name="v_bf0", align_bytes=64),
             values.tile([P, N], BF16, name="v_bf1", align_bytes=64, offset=2 * V_BYTES + 2048),
             keep.tile([P, N], BF16, name="v_bf2", align_bytes=64),
             keep.tile([P, N], BF16, name="v_bf3", align_bytes=64),
         ]
-        picks = []
 
         def gather_values(c):
-            picked = keep.tile([P, N], BF16, name="v_picked%d" % c)
-            picks.append(picked)
+            picked = keep.tile([P, N], BF16, name="v_picked%d" % c, tag="picked%d" % c)
             nc.vector.tensor_copy(picked[:], v_pool[c][:].indirect(offsets[:]))
-
-        def turn_values(c):
-            words = picks[c][:].bitcast(F32)
-            turned = psum.tile([P, 2, P], F32, name="v_turned", tag="bank%d" % (7, 3, 6, 7)[c], bufs=1)
+            words = picked[:].bitcast(F32)
+            turned = psum.tile([P, 2, P], F32, name="v_turned", tag="turned", bufs=3)
             for u in range(2):
                 nc.tensor.transpose(turned[:, u, :], words[:, u : N // 2 : 2], ident[:])
+            return turned
+
+        def interleave_values(c, turned):
             nc.scalar.copy(
-                v_bf[c][:].bitcast(F32).rearrange("p (e u) -> p e u", u=2),
-                turned[:].rearrange("p u e -> p e u"),
+                v_bf[c][:].bitcast(F32).rearrange("p (e u) -> p e u", u=2), turned[:].rearrange("p u e -> p e u")
             )
 
         def quantize_values(c, codes, scale):
             nc.vector.quantize_mx(out=codes.bitcast(FP8X4), scales=scale, in_=v_bf[c][:])
 
-        def multiply(dest, j, codes, scale):
-            cols = slice(j * P, (j + 1) * P)
+        def scores(bank, j, s):
+            cols = slice((j % 2) * P, (j % 2 + 1) * P)
+            slots = slice(s * N // 2, (s + 1) * N // 2)
             nc.tensor.matmul_mx(
-                out=dest,
-                lhsT=y_codes[:, cols].bitcast(FP8X4),
-                lhsT_scale=y_scale[:, cols],
-                rhs=codes.bitcast(FP8X4),
-                rhs_scale=scale,
+                out=bank[:, slots],
+                lhsT=q_codes[j // 2][:, cols].bitcast(FP8X4),
+                lhsT_scale=q_scale[j // 2][:, cols],
+                rhs=k_codes[s][:].bitcast(FP8X4),
+                rhs_scale=k_scale[:, slots],
                 start=True,
                 stop=True,
             )
 
+        def exponentials(bank, j):
+            expd = keep.tile([P, N], F32, name="expd%d" % j)
+            if j == 0:
+                dest, source = expd[:].rearrange("m (t p) -> m t p", t=PACK), bank[:].rearrange("m (p t) -> m t p", t=PACK)
+            else:
+                dest = expd[:].rearrange("m (u p h) -> m u p h", u=2, h=2)
+                source = bank[:].rearrange("m (p u h) -> m u p h", u=2, h=2)
+            nc.scalar.activation(
+                dest,
+                source,
+                EXP,
+                bias=neg_ls[:, j : j + 1],
+                scale=1.0,
+            )
+            return expd
+
+        def weights_on_scalar(expd):
+            turned = psum.tile([P, PACK, P], F32, name="exp_turned", tag="mx", bufs=4)
+            planes = keep.tile([P, PACK, P], BF16, name="y_planes", tag="picked0")
+            for t in range(PACK):
+                nc.tensor.transpose(turned[:, t, :], expd[:, t * P : (t + 1) * P], ident[:])
+            for t in range(PACK):
+                nc.scalar.activation(planes[:, t, :], turned[:, t, :], COPY, scale=us_sb[:, t : t + 1])
+            nc.scalar.copy(y_bf[:, 0:N].rearrange("p (m t) -> p m t", t=PACK), planes[:].rearrange("p t m -> p m t"))
+
+        def weights(tiles, expd):
+            turned = psum.tile([P, len(tiles), 2, P], F32, name="y_turned", tag="turned", bufs=3)
+            for i, j in enumerate(tiles):
+                rounded = values.tile([P, N], BF16, name="y_rounded%d" % j, offset=j * N * 2)
+                engine, factor = (
+                    (nc.gpsimd, us_rows_sb[:]) if j == 1 else (nc.vector, us_rows[:].rearrange("m (u h) p -> m u p h", u=2))
+                )
+                engine.tensor_tensor(
+                    rounded[:].rearrange("m (u p h) -> m u p h", u=2, h=2),
+                    expd[j][:].rearrange("m (u p h) -> m u p h", u=2, h=2),
+                    factor,
+                    MULT,
+                )
+                words = rounded[:].bitcast(F32)
+                for u in range(2):
+                    nc.tensor.transpose(turned[:, i, u, :], words[:, u * P : (u + 1) * P], ident[:])
+            nc.scalar.copy(
+                y_bf[:, tiles[0] * N : (tiles[-1] + 1) * N].bitcast(F32).rearrange("p (i m u) -> p i m u", m=P, u=2),
+                turned[:].rearrange("p i u m -> p i m u"),
+            )
+
         out_rows = out[0].rearrange("(m j) e -> m j e", j=q_tiles)
 
-        gather_values(0)
-        turn_values(0)
-        for j in (0, 2, 3, 1):
-            weights(j)
+        def product(first, codes, scale, tiles_a_bank, engines):
+            width = codes.shape[1]
+            cols = slice(first * P, first * P + width)
+            for half, j0 in enumerate(range(0, q_tiles, tiles_a_bank)):
+                bank = psum.tile([P, tiles_a_bank, width], F32, name="product", tag="mx", bufs=4)
+                for j in range(j0, j0 + tiles_a_bank):
+                    multiply(bank[:, j - j0, :], j, codes, scale)
+                copy, queue, offset = engines[half]
+                result = values.tile([P, tiles_a_bank, width], F32, name="result%d_%d" % (first, half), offset=offset)
+                copy(result[:], bank[:])
+                queue.dma_start(out_rows[:, j0 : j0 + tiles_a_bank, cols], result[:])
+
+        def multiply(dest, j, codes, scale):
+            nc.tensor.matmul_mx(
+                out=dest,
+                lhsT=y_codes[:, j * P : (j + 1) * P].bitcast(FP8X4),
+                lhsT_scale=y_scale[:, j * P : (j + 1) * P],
+                rhs=codes[:].bitcast(FP8X4),
+                rhs_scale=scale[:],
+                start=True,
+                stop=True,
+            )
+
+        banks = [psum.tile([P, N], F32, name="scores%d" % j, tag="mx", bufs=4) for j in range(q_tiles)]
+        for pair in range(2):
+            for s in range(2):
+                for j in (2 * pair, 2 * pair + 1):
+                    scores(banks[j], j, s)
+        expd = [exponentials(banks[j], j) for j in range(q_tiles)]
+        interleave_values(0, gather_values(0))
+        weights_on_scalar(expd[0])
+        weights((2, 3), expd)
+        weights((1,), expd)
         codes = keep.tile([P, 2 * P], U32, name="v_codes01", align_bytes=64)
         scale = keep.tile([P, 2 * P], U8, name="v_scale01", align_bytes=64)
         quantize_values(0, codes[:, 0:P], scale[:, 0:P])
-        gather_values(1)
-        gather_values(2)
-        turn_values(1)
-        turn_values(2)
+        turned1 = gather_values(1)
+        warm = psum.tile([P, N], F32, name="warm", tag="turned", bufs=3)
+        for j in range(2):
+            for s in range(2):
+                scores(warm, j, s)
+        turned2 = gather_values(2)
+        interleave_values(1, turned1)
+        interleave_values(2, turned2)
         nc.vector.quantize_mx(out=y_codes[:].bitcast(FP8X4), scales=y_scale[:], in_=y_bf[:])
         quantize_values(1, codes[:, P : 2 * P], scale[:, P : 2 * P])
-        for c in range(2):
-            bank = psum.tile([P, q_tiles, P], F32, name="early_product", tag="bank%d" % (4, 1)[c], bufs=1)
-            for j in range(q_tiles):
-                multiply(bank[:, j, :], j, codes[:, c * P : (c + 1) * P], scale[:, c * P : (c + 1) * P])
-            early = keep.tile([P, q_tiles, P], F32, name="early%d" % c)
-            nc.scalar.copy(early[:], bank[:])
-            nc.sync.dma_start(out_rows[:, :, c * P : (c + 1) * P], early[:])
-        gather_values(3)
-        turn_values(3)
+        turned3 = gather_values(3)
+        interleave_values(3, turned3)
+        product(0, codes, scale, 1, [(nc.scalar.copy, nc.sync, V_BYTES + 1024 * j) for j in range(q_tiles)])
         codes = values.tile([P, P], U32, name="v_codes2", align_bytes=64, offset=3 * V_BYTES)
         scale = keep.tile([P, P], U8, name="v_scale2", align_bytes=64)
         quantize_values(2, codes[:], scale[:])
-        for h in range(2):
-            bank = psum.tile([P, 2, P], F32, name="second_product", tag="bank%d" % (5, 0)[h], bufs=1)
-            for i in range(2):
-                multiply(bank[:, i, :], 2 * h + i, codes[:], scale[:])
-            second = keep.tile([P, 2, P], F32, name="second%d" % h)
-            (nc.vector.tensor_copy, nc.scalar.copy)[h](second[:], bank[:])
-            nc.sync.dma_start(out_rows[:, 2 * h : 2 * h + 2, 2 * P : 3 * P], second[:])
+        product(2, codes, scale, 2, [(nc.vector.tensor_copy, nc.sync, 4096), (nc.scalar.copy, nc.sync, 6144)])
         codes = keep.tile([P, P], U32, name="v_codes3", align_bytes=64)
         scale = keep.tile([P, P], U8, name="v_scale3", align_bytes=64)
         quantize_values(3, codes[:], scale[:])
-        last = keep.tile([P, q_tiles, P], F32, name="last")
+        last = values.tile([P, q_tiles, P], F32, name="last", offset=V_BYTES + 4096)
         for j in range(q_tiles):
-            bank = psum.tile([P, P], F32, name="last_product", tag="bank%d" % (3, 4, 1, 2)[j], bufs=1)
-            multiply(bank[:], j, codes[:], scale[:])
-            (nc.vector.tensor_copy, nc.scalar.copy)[j % 2](last[:, j, :], bank[:])
-            (nc.sync, nc.scalar)[j % 2].dma_start(out_rows[:, j, 3 * P :], last[:, j, :])
+            bank = psum.tile([P, P], F32, name="last_product", tag=("turned", "mx")[j % 2], bufs=(3, 4)[j % 2])
+            multiply(bank[:], j, codes, scale)
+            (nc.scalar.copy, nc.vector.tensor_copy)[j % 2](last[:, j, :], bank[:])
+            (nc.scalar, nc.sync)[j % 2].dma_start(out_rows[:, j, 3 * P :], last[:, j, :])

@@ -95,11 +95,14 @@ def tile_attend_at_lse_topk_kernel(tc, qT, k_words, k_scales, vT, ls, us, offs, 
 
         def gather_values(c):
             picked = keep.tile([P, N], BF16, name="v_picked%d" % c, tag="picked%d" % c)
-            nc.vector.tensor_copy(picked[:], v_pool[c][:].indirect(offsets[:]))
+            last_block = c == v_blocks - 1
+            dest = picked[:].rearrange("p (u s h) -> p s u h", u=2, h=2) if last_block else picked[:]
+            nc.vector.tensor_copy(dest, v_pool[c][:].indirect(offsets[:]))
             words = picked[:].bitcast(F32)
             turned = psum.tile([P, 2, P], F32, name="v_turned", tag="turned", bufs=3)
             for u in range(2):
-                nc.tensor.transpose(turned[:, u, :], words[:, u : N // 2 : 2], ident[:])
+                source = words[:, u * P : (u + 1) * P] if last_block else words[:, u : N // 2 : 2]
+                nc.tensor.transpose(turned[:, u, :], source, ident[:])
             return turned
 
         def interleave_values(c, turned):

@@ -11,6 +11,7 @@ U16 = mybir.dt.uint16
 U8 = mybir.dt.uint8
 FP8X4 = mybir.dt.float8_e4m3fn_x4
 MULT = mybir.AluOpType.mult
+ADD = mybir.AluOpType.add
 COPY = mybir.ActivationFunctionType.Copy
 EXP = mybir.ActivationFunctionType.Exp
 
@@ -18,8 +19,9 @@ P = 128
 PACK = 4
 T, N, D, NQ, DV = 2048, 512, 512, 512, 512
 V_BYTES = T * 4
-GROUPS = ((0, 2), (2, 1), (3, 1))
+LIST_COLS = N // 16
 FLOPS = 2 * D * N * NQ + 2 * N * NQ * DV
+ON_VECTOR = (32, 0, 16, 16)
 
 
 def tile_attend_at_lse_topk_kernel(tc, qT, k_words, k_scales, vT, ls, us, offs, out):
@@ -29,22 +31,25 @@ def tile_attend_at_lse_topk_kernel(tc, qT, k_words, k_scales, vT, ls, us, offs, 
     with ExitStack() as ctx:
         keep = ctx.enter_context(tc.tile_pool(name="keep", bufs=1))
         values = ctx.enter_context(tc.tile_pool(name="values", bufs=1))
-        psum = ctx.enter_context(tc.psum_pool(name="psum", bufs=2))
+        psum = ctx.enter_context(tc.psum_pool(name="psum", bufs=1))
+
+        def bank(number, shape, name):
+            return psum.tile(shape, F32, name=name, tag="bank%d" % number)
 
         q_raw = keep.tile([P, PACK, NQ], F32, name="q_raw")
         nc.sync.dma_start(q_raw[:], qT[0].rearrange("(p r) q -> p r q", r=PACK))
-        offsets = keep.tile([P, N // 16], U16, name="offsets")
+        offsets = keep.tile([P, LIST_COLS], U16, name="offsets")
         nc.sync.dma_start(offsets[:], offs)
-        us_sb = keep.tile([P, PACK], F32, name="us_sb")
-        nc.sync.dma_start(us_sb[:], us[0].rearrange("(p t) o -> p (t o)", t=PACK))
-        k_scale_pool = values.tile([P, T], U8, name="k_scale_pool", offset=(v_blocks + 1) * V_BYTES)
+        ls_sb = keep.tile([P, q_tiles], F32, name="ls_sb")
+        nc.sync.dma_start(ls_sb[:], ls[0, 0].rearrange("(m j) -> m j", j=q_tiles))
+        k_scale_pool = values.tile([P, T], U8, name="k_scale_pool", offset=v_blocks * V_BYTES)
         nc.vector.memset(k_scale_pool[:].bitcast(I32), 0)
         for r in range(4):
             nc.sync.dma_start(k_scale_pool[r:P:32, :].bitcast(I32), k_scales[0, r:16:4, :].bitcast(I32))
-        k_word_pool = values.tile([P, T], I32, name="k_word_pool", offset=v_blocks * V_BYTES)
+        k_word_pool = values.tile([P, T], I32, name="k_word_pool", offset=(v_blocks + 1) * V_BYTES)
         nc.sync.dma_start(k_word_pool[:], k_words[0].rearrange("p t r -> p (t r)").bitcast(I32))
-        ls_sb = keep.tile([P, q_tiles], F32, name="ls_sb")
-        nc.sync.dma_start(ls_sb[:], ls[0, 0].rearrange("(m j) -> m j", j=q_tiles))
+        us_sb = keep.tile([P, PACK], F32, name="us_sb")
+        nc.sync.dma_start(us_sb[:], us[0].rearrange("(p t) o -> p (t o)", t=PACK))
         v_pool = []
         for c in range(v_blocks):
             block = values.tile([P, T], F32, name="v_pool%d" % c, offset=c * V_BYTES)
@@ -53,186 +58,157 @@ def tile_attend_at_lse_topk_kernel(tc, qT, k_words, k_scales, vT, ls, us, offs, 
 
         ident = keep.tile([P, P], F32, name="ident")
         make_identity(nc, ident[:])
-
-        us_rows = psum.tile([P, PACK, P], F32, name="us_rows", bufs=1)
-        for t in range(PACK):
-            nc.tensor.transpose(us_rows[:, t, :], us_sb[:, t : t + 1].to_broadcast([P, P]), ident[:])
-        us_rows_sb = keep.tile([P, 2, P, 2], F32, name="us_rows_sb")
-        nc.scalar.activation(us_rows_sb[:], us_rows[:].rearrange("m (u h) p -> m u p h", u=2), COPY)
+        neg_ls = keep.tile([P, q_tiles], F32, name="neg_ls")
 
         q_rows = q_raw[:].rearrange("p r (m j) -> p m r j", j=q_tiles)
-        q_bf = []
-        for h in range(2):
-            pair = keep.tile([P, 2 * N], BF16, name="q_bf%d" % h, align_bytes=64)
-            nc.scalar.copy(pair[:].rearrange("p (j m r) -> p m r j", j=2, r=PACK), q_rows[:, :, :, 2 * h : 2 * h + 2])
-            q_bf.append(pair)
-        neg_ls = keep.tile([P, q_tiles], F32, name="neg_ls")
-        nc.scalar.activation(neg_ls[:], ls_sb[:], COPY, scale=-1.0)
+        q_bf = [
+            values.tile([P, 2 * N], BF16, name="q_bf%d" % h, align_bytes=64, offset=(v_blocks + 2) * V_BYTES + 2048 * h)
+            for h in range(2)
+        ]
+        nc.scalar.copy(q_bf[0][:].rearrange("p (j m r) -> p m r j", j=2, r=PACK), q_rows[:, :, :, 0:2])
+        second_pair = q_bf[1][:].rearrange("p (j m r) -> p m r j", j=2, r=PACK)
+        nc.vector.tensor_copy(second_pair[:, P // 2 :], q_rows[:, P // 2 :, :, 2:4])
+        nc.scalar.copy(second_pair[:, : P // 2], q_rows[:, : P // 2, :, 2:4])
+        nc.gpsimd.tensor_scalar(neg_ls[:], ls_sb[:], -1.0, 0.0, MULT, ADD)
         k_scale = keep.tile([P, N], U8, name="k_scale", align_bytes=64)
         nc.vector.tensor_copy(k_scale[:], k_scale_pool[:].indirect(offsets[:]))
-        q_codes = [
-            values.tile([P, 2 * P], U32, name="q_codes0", align_bytes=64, offset=(v_blocks + 1) * V_BYTES),
-            values.tile([P, 2 * P], U32, name="q_codes1", align_bytes=64, offset=v_blocks * V_BYTES),
+        q_codes = [keep.tile([P, 2 * P], U32, name="q_codes%d" % h, align_bytes=64) for h in range(2)]
+        q_scale = [
+            values.tile([P, 2 * P], U8, name="q_scale%d" % h, align_bytes=64, offset=v_blocks * V_BYTES + 256 * h)
+            for h in range(2)
         ]
-        q_scale = [keep.tile([P, 2 * P], U8, name="q_scale%d" % h, align_bytes=64) for h in range(2)]
-        nc.vector.quantize_mx(out=q_codes[0][:].bitcast(FP8X4), scales=q_scale[0][:], in_=q_bf[0][:])
+        for h in range(2):
+            nc.vector.quantize_mx(out=q_codes[h][:].bitcast(FP8X4), scales=q_scale[h][:], in_=q_bf[h][:])
         k_codes = []
         for s in range(2):
-            picked_words = keep.tile([P, N // 2], U32, name="k_codes%d" % s, align_bytes=64)
+            picked_words = values.tile(
+                [P, N // 2], U32, name="k_codes%d" % s, align_bytes=64, offset=(v_blocks + 2) * V_BYTES + 1536 + 1024 * s
+            )
             nc.vector.tensor_copy(picked_words[:], k_word_pool[:].bitcast(U32).indirect(offsets[:, s * 16 : (s + 1) * 16]))
             k_codes.append(picked_words)
-        nc.vector.quantize_mx(out=q_codes[1][:].bitcast(FP8X4), scales=q_scale[1][:], in_=q_bf[1][:])
 
-        y_codes = values.tile([P, NQ], U32, name="y_codes", align_bytes=64, offset=2 * V_BYTES)
-        y_scale = keep.tile([P, NQ], U8, name="y_scale", align_bytes=64)
-        y_bf = keep.tile([P, NQ * PACK], BF16, name="y_bf", align_bytes=64)
-        v_bf = [
-            keep.tile([P, N], BF16, name="v_bf0", align_bytes=64),
-            values.tile([P, N], BF16, name="v_bf1", align_bytes=64, offset=2 * V_BYTES + 2048),
-            keep.tile([P, N], BF16, name="v_bf2", align_bytes=64),
-            keep.tile([P, N], BF16, name="v_bf3", align_bytes=64),
-        ]
-
-        def gather_values(c):
-            picked = keep.tile([P, N], BF16, name="v_picked%d" % c, tag="picked%d" % c)
-            last_block = c == v_blocks - 1
-            dest = picked[:].rearrange("p (u s h) -> p s u h", u=2, h=2) if last_block else picked[:]
-            nc.vector.tensor_copy(dest, v_pool[c][:].indirect(offsets[:]))
-            words = picked[:].bitcast(F32)
-            turned = psum.tile([P, 2, P], F32, name="v_turned", tag="turned", bufs=3)
-            for u in range(2):
-                source = words[:, u * P : (u + 1) * P] if last_block else words[:, u : N // 2 : 2]
-                nc.tensor.transpose(turned[:, u, :], source, ident[:])
-            return turned
-
-        def interleave_values(c, turned):
-            nc.scalar.copy(
-                v_bf[c][:].bitcast(F32).rearrange("p (e u) -> p e u", u=2), turned[:].rearrange("p u e -> p e u")
-            )
-
-        def quantize_values(c, codes, scale):
-            nc.vector.quantize_mx(out=codes.bitcast(FP8X4), scales=scale, in_=v_bf[c][:])
-
-        def scores(bank, j, s):
+        def scores(dest, j, s):
             cols = slice((j % 2) * P, (j % 2 + 1) * P)
-            slots = slice(s * N // 2, (s + 1) * N // 2)
             nc.tensor.matmul_mx(
-                out=bank[:, slots],
+                out=dest,
                 lhsT=q_codes[j // 2][:, cols].bitcast(FP8X4),
                 lhsT_scale=q_scale[j // 2][:, cols],
                 rhs=k_codes[s][:].bitcast(FP8X4),
-                rhs_scale=k_scale[:, slots],
+                rhs_scale=k_scale[:, s * N // 2 : (s + 1) * N // 2],
                 start=True,
                 stop=True,
             )
 
-        def exponentials(bank, j):
-            expd = keep.tile([P, N], F32, name="expd%d" % j)
-            if j == 0:
-                dest, source = expd[:].rearrange("m (t p) -> m t p", t=PACK), bank[:].rearrange("m (p t) -> m t p", t=PACK)
+        def exponentials(dest, source, j):
+            source = source.rearrange("m (p t) -> m t p", t=PACK)
+            nc.scalar.activation(dest, source, EXP, bias=neg_ls[:, j : j + 1], scale=1.0)
+
+        expd = [keep.tile([P, PACK, P], F32, name="expd%d" % j) for j in range(q_tiles)]
+        for s in range(2):
+            for j in range(2):
+                sums = bank(2 * s + j, [P, N // 2], "scores%d_%d" % (j, s))
+                scores(sums[:], j, s)
+                exponentials(expd[j][:, :, s * P // 2 : (s + 1) * P // 2], sums[:], j)
+        for j in range(2, q_tiles):
+            sums = bank(3 + j, [P, N], "scores%d" % j)
+            for s in range(2):
+                scores(sums[:, s * N // 2 : (s + 1) * N // 2], j, s)
+            exponentials(expd[j][:], sums[:], j)
+
+        y_bf = [values.tile([P, 2 * N], BF16, name="y_bf%d" % h, align_bytes=64, offset=2048 * h) for h in range(2)]
+        y_codes = [keep.tile([P, 2 * P], U32, name="y_codes%d" % h, align_bytes=64) for h in range(2)]
+        y_scale = [keep.tile([P, 2 * P], U8, name="y_scale%d" % h, align_bytes=64) for h in range(2)]
+        us_spread = us_sb[:].unsqueeze(1).to_broadcast([P, P, PACK])
+
+        def weights(j):
+            turned = bank((4, 7, 0, 1)[j], [P, PACK, P], "y_turned%d" % j)
+            for t in range(PACK):
+                nc.tensor.transpose(turned[:, t, :], expd[j][:, t, :], ident[:])
+            dest = y_bf[j // 2][:, (j % 2) * N : (j % 2 + 1) * N].rearrange("p (m t) -> p m t", t=PACK)
+            nc.vector.tensor_tensor(dest, turned[:].rearrange("p t m -> p m t"), us_spread, MULT)
+
+        def quantize_weights(h):
+            nc.vector.quantize_mx(out=y_codes[h][:].bitcast(FP8X4), scales=y_scale[h][:], in_=y_bf[h][:])
+
+        def gather_values(c):
+            picked = keep.tile([P, N], BF16, name="v_picked%d" % c)
+            cut = ON_VECTOR[c]
+            if cut > 0:
+                nc.vector.tensor_copy(picked[:, : 16 * cut], v_pool[c][:].indirect(offsets[:, :cut]))
+            if cut < LIST_COLS:
+                nc.scalar.activation(picked[:, 16 * cut :], v_pool[c][:].indirect(offsets[:, cut:]), COPY)
+            return picked
+
+        def turn_values(c, picked):
+            words = picked[:].bitcast(F32)
+            turned = bank((2, 3, 5, 6)[c], [P, 2, P], "v_turned%d" % c)
+            for u in range(2):
+                nc.tensor.transpose(turned[:, u, :], words[:, u : N // 2 : 2], ident[:])
+            if c in (0, 2):
+                v_bf = values.tile([P, N], BF16, name="v_bf%d" % c, align_bytes=64, offset=(c + 1) * V_BYTES + 1024)
             else:
-                dest = expd[:].rearrange("m (u p h) -> m u p h", u=2, h=2)
-                source = bank[:].rearrange("m (p u h) -> m u p h", u=2, h=2)
-            nc.scalar.activation(
-                dest,
-                source,
-                EXP,
-                bias=neg_ls[:, j : j + 1],
-                scale=1.0,
-            )
-            return expd
+                v_bf = keep.tile([P, N], BF16, name="v_bf%d" % c, align_bytes=64)
+            nc.scalar.copy(v_bf[:].bitcast(F32).rearrange("p (e u) -> p e u", u=2), turned[:].rearrange("p u e -> p e u"))
+            return v_bf
 
-        def weights_on_scalar(expd):
-            turned = psum.tile([P, PACK, P], F32, name="exp_turned", tag="mx", bufs=4)
-            planes = keep.tile([P, PACK, P], BF16, name="y_planes", tag="picked0")
-            for t in range(PACK):
-                nc.tensor.transpose(turned[:, t, :], expd[:, t * P : (t + 1) * P], ident[:])
-            for t in range(PACK):
-                nc.scalar.activation(planes[:, t, :], turned[:, t, :], COPY, scale=us_sb[:, t : t + 1])
-            nc.scalar.copy(y_bf[:, 0:N].rearrange("p (m t) -> p m t", t=PACK), planes[:].rearrange("p t m -> p m t"))
-
-        def weights(tiles, expd):
-            turned = psum.tile([P, len(tiles), 2, P], F32, name="y_turned", tag="turned", bufs=3)
-            for i, j in enumerate(tiles):
-                rounded = values.tile([P, N], BF16, name="y_rounded%d" % j, offset=j * N * 2)
-                engine, factor = (
-                    (nc.gpsimd, us_rows_sb[:]) if j == 1 else (nc.vector, us_rows[:].rearrange("m (u h) p -> m u p h", u=2))
-                )
-                engine.tensor_tensor(
-                    rounded[:].rearrange("m (u p h) -> m u p h", u=2, h=2),
-                    expd[j][:].rearrange("m (u p h) -> m u p h", u=2, h=2),
-                    factor,
-                    MULT,
-                )
-                words = rounded[:].bitcast(F32)
-                for u in range(2):
-                    nc.tensor.transpose(turned[:, i, u, :], words[:, u * P : (u + 1) * P], ident[:])
-            nc.scalar.copy(
-                y_bf[:, tiles[0] * N : (tiles[-1] + 1) * N].bitcast(F32).rearrange("p (i m u) -> p i m u", m=P, u=2),
-                turned[:].rearrange("p i u m -> p i m u"),
-            )
+        def quantize_values(c, v_bf):
+            nc.vector.quantize_mx(out=v_codes[c][:].bitcast(FP8X4), scales=v_scale[c][:], in_=v_bf[:])
 
         out_rows = out[0].rearrange("(m j) e -> m j e", j=q_tiles)
 
-        def product(first, codes, scale, tiles_a_bank, engines):
-            width = codes.shape[1]
-            cols = slice(first * P, first * P + width)
-            for half, j0 in enumerate(range(0, q_tiles, tiles_a_bank)):
-                bank = psum.tile([P, tiles_a_bank, width], F32, name="product", tag="mx", bufs=4)
-                for j in range(j0, j0 + tiles_a_bank):
-                    multiply(bank[:, j - j0, :], j, codes, scale)
-                copy, queue, offset = engines[half]
-                result = values.tile([P, tiles_a_bank, width], F32, name="result%d_%d" % (first, half), offset=offset)
-                copy(result[:], bank[:])
-                queue.dma_start(out_rows[:, j0 : j0 + tiles_a_bank, cols], result[:])
-
         def multiply(dest, j, codes, scale):
+            cols = slice((j % 2) * P, (j % 2 + 1) * P)
             nc.tensor.matmul_mx(
                 out=dest,
-                lhsT=y_codes[:, j * P : (j + 1) * P].bitcast(FP8X4),
-                lhsT_scale=y_scale[:, j * P : (j + 1) * P],
-                rhs=codes[:].bitcast(FP8X4),
-                rhs_scale=scale[:],
+                lhsT=y_codes[j // 2][:, cols].bitcast(FP8X4),
+                lhsT_scale=y_scale[j // 2][:, cols],
+                rhs=codes.bitcast(FP8X4),
+                rhs_scale=scale,
                 start=True,
                 stop=True,
             )
 
-        banks = [psum.tile([P, N], F32, name="scores%d" % j, tag="mx", bufs=4) for j in range(q_tiles)]
-        for pair in range(2):
-            for s in range(2):
-                for j in (2 * pair, 2 * pair + 1):
-                    scores(banks[j], j, s)
-        expd = [exponentials(banks[j], j) for j in range(q_tiles)]
-        interleave_values(0, gather_values(0))
-        weights_on_scalar(expd[0])
-        weights((2, 3), expd)
-        weights((1,), expd)
-        codes = keep.tile([P, 2 * P], U32, name="v_codes01", align_bytes=64)
-        scale = keep.tile([P, 2 * P], U8, name="v_scale01", align_bytes=64)
-        quantize_values(0, codes[:, 0:P], scale[:, 0:P])
-        turned1 = gather_values(1)
-        warm = psum.tile([P, N], F32, name="warm", tag="turned", bufs=3)
-        for j in range(2):
-            for s in range(2):
-                scores(warm, j, s)
-        turned2 = gather_values(2)
-        interleave_values(1, turned1)
-        interleave_values(2, turned2)
-        nc.vector.quantize_mx(out=y_codes[:].bitcast(FP8X4), scales=y_scale[:], in_=y_bf[:])
-        quantize_values(1, codes[:, P : 2 * P], scale[:, P : 2 * P])
-        turned3 = gather_values(3)
-        interleave_values(3, turned3)
-        product(0, codes, scale, 1, [(nc.scalar.copy, nc.sync, V_BYTES + 1024 * j) for j in range(q_tiles)])
-        codes = values.tile([P, P], U32, name="v_codes2", align_bytes=64, offset=3 * V_BYTES)
-        scale = keep.tile([P, P], U8, name="v_scale2", align_bytes=64)
-        quantize_values(2, codes[:], scale[:])
-        product(2, codes, scale, 2, [(nc.vector.tensor_copy, nc.sync, 4096), (nc.scalar.copy, nc.sync, 6144)])
-        codes = keep.tile([P, P], U32, name="v_codes3", align_bytes=64)
-        scale = keep.tile([P, P], U8, name="v_scale3", align_bytes=64)
-        quantize_values(3, codes[:], scale[:])
-        last = values.tile([P, q_tiles, P], F32, name="last", offset=V_BYTES + 4096)
+        def product(c, banks, copies, offset):
+            tiles_a_bank = q_tiles // len(banks)
+            for h, number in enumerate(banks):
+                sums = bank(number, [P, tiles_a_bank, P], "product%d_%d" % (c, h))
+                first = h * tiles_a_bank
+                for i in range(tiles_a_bank):
+                    multiply(sums[:, i, :], first + i, v_codes[c][:], v_scale[c][:])
+                result = values.tile([P, tiles_a_bank, P], F32, name="result%d_%d" % (c, h), offset=offset + 1024 * h)
+                copies[h](result[:], sums[:])
+                nc.sync.dma_start(out_rows[:, first : first + tiles_a_bank, c * P : (c + 1) * P], result[:])
+
+        v_codes = [
+            keep.tile([P, P], U32, name="v_codes0", align_bytes=64),
+            values.tile([P, P], U32, name="v_codes1", align_bytes=64, offset=2 * V_BYTES),
+            values.tile([P, P], U32, name="v_codes2", align_bytes=64, offset=3 * V_BYTES),
+            keep.tile([P, P], U32, name="v_codes3", align_bytes=64),
+        ]
+        v_scale = [keep.tile([P, P], U8, name="v_scale%d" % c, align_bytes=64) for c in range(v_blocks)]
+
+        picked = gather_values(0)
         for j in range(q_tiles):
-            bank = psum.tile([P, P], F32, name="last_product", tag=("turned", "mx")[j % 2], bufs=(3, 4)[j % 2])
-            multiply(bank[:], j, codes, scale)
-            (nc.scalar.copy, nc.vector.tensor_copy)[j % 2](last[:, j, :], bank[:])
+            weights(j)
+        picked1 = gather_values(1)
+        v_bf0 = turn_values(0, picked)
+        quantize_weights(0)
+        quantize_weights(1)
+        quantize_values(0, v_bf0)
+        v_bf1 = turn_values(1, picked1)
+        picked2 = gather_values(2)
+        quantize_values(1, v_bf1)
+        product(0, (4,), (nc.vector.tensor_copy,), 2 * V_BYTES + 2048)
+        v_bf2 = turn_values(2, picked2)
+        picked3 = gather_values(3)
+        quantize_values(2, v_bf2)
+        product(1, (7,), (nc.vector.tensor_copy,), 3 * V_BYTES + 2048)
+        v_bf3 = turn_values(3, picked3)
+        quantize_values(3, v_bf3)
+        product(2, (0, 1), (nc.vector.tensor_copy, nc.scalar.copy), 4096)
+        last = keep.tile([P, q_tiles, P], F32, name="last")
+        for j in range(q_tiles):
+            sums = bank((2, 3, 4, 5)[j], [P, P], "last_product%d" % j)
+            multiply(sums[:], j, v_codes[3][:], v_scale[3][:])
+            (nc.scalar.copy, nc.vector.tensor_copy)[j % 2](last[:, j, :], sums[:])
             (nc.scalar, nc.sync)[j % 2].dma_start(out_rows[:, j, 3 * P :], last[:, j, :])

@@ -36,18 +36,20 @@ def tile_attend_at_lse_topk_kernel(tc, qT, k_words, k_scales, vT, ls, us, offs, 
         def bank(number, shape, name):
             return psum.tile(shape, F32, name=name, tag="bank%d" % number)
 
-        q_raw = keep.tile([P, PACK, NQ], F32, name="q_raw")
-        nc.sync.dma_start(q_raw[:], qT[0].rearrange("(p r) q -> p r q", r=PACK))
+        q_halves = qT[0].rearrange("(p r) (h q) -> h p r q", r=PACK, h=2)
+        q_raw = [keep.tile([P, PACK, NQ // 2], F32, name="q_raw%d" % h) for h in range(2)]
+        nc.sync.dma_start(q_raw[0][:], q_halves[0])
         offsets = keep.tile([P, LIST_COLS], U16, name="offsets")
         nc.sync.dma_start(offsets[:], offs)
         ls_sb = keep.tile([P, q_tiles], F32, name="ls_sb")
-        nc.sync.dma_start(ls_sb[:], ls[0, 0].rearrange("(m j) -> m j", j=q_tiles))
+        nc.sync.dma_start(ls_sb[:].rearrange("m (h i) -> m h i", h=2), ls[0, 0].rearrange("(h m i) -> m h i", h=2, i=2))
         k_scale_pool = values.tile([P, T], U8, name="k_scale_pool", offset=v_blocks * V_BYTES)
         nc.vector.memset(k_scale_pool[:].bitcast(I32), 0)
         for r in range(4):
             nc.sync.dma_start(k_scale_pool[r:P:32, :].bitcast(I32), k_scales[0, r:16:4, :].bitcast(I32))
         k_word_pool = values.tile([P, T], I32, name="k_word_pool", offset=(v_blocks + 1) * V_BYTES)
         nc.sync.dma_start(k_word_pool[:], k_words[0].rearrange("p t r -> p (t r)").bitcast(I32))
+        nc.sync.dma_start(q_raw[1][:], q_halves[1])
         us_sb = keep.tile([P, PACK], F32, name="us_sb")
         nc.sync.dma_start(us_sb[:], us[0].rearrange("(p t) o -> p (t o)", t=PACK))
         v_pool = []
@@ -58,18 +60,16 @@ def tile_attend_at_lse_topk_kernel(tc, qT, k_words, k_scales, vT, ls, us, offs, 
 
         ident = keep.tile([P, P], F32, name="ident")
         make_identity(nc, ident[:])
-        neg_ls = keep.tile([P, q_tiles], F32, name="neg_ls")
+        neg_ls_first = keep.tile([P, 2], F32, name="neg_ls_first")
 
-        q_rows = q_raw[:].rearrange("p r (m j) -> p m r j", j=q_tiles)
+        q_rows = [half[:].rearrange("p r (m i) -> p m r i", i=2) for half in q_raw]
         q_bf = [
             values.tile([P, 2 * N], BF16, name="q_bf%d" % h, align_bytes=64, offset=(v_blocks + 2) * V_BYTES + 2048 * h)
             for h in range(2)
         ]
-        nc.scalar.copy(q_bf[0][:].rearrange("p (j m r) -> p m r j", j=2, r=PACK), q_rows[:, :, :, 0:2])
+        nc.scalar.copy(q_bf[0][:].rearrange("p (j m r) -> p m r j", j=2, r=PACK), q_rows[0])
         second_pair = q_bf[1][:].rearrange("p (j m r) -> p m r j", j=2, r=PACK)
-        nc.vector.tensor_copy(second_pair[:, P // 2 :], q_rows[:, P // 2 :, :, 2:4])
-        nc.scalar.copy(second_pair[:, : P // 2], q_rows[:, : P // 2, :, 2:4])
-        nc.gpsimd.tensor_scalar(neg_ls[:], ls_sb[:], -1.0, 0.0, MULT, ADD)
+        nc.gpsimd.tensor_scalar(neg_ls_first[:], ls_sb[:, 0:2], -1.0, 0.0, MULT, ADD)
         k_scale = keep.tile([P, N], U8, name="k_scale", align_bytes=64)
         nc.vector.tensor_copy(k_scale[:], k_scale_pool[:].indirect(offsets[:]))
         q_codes = [keep.tile([P, 2 * P], U32, name="q_codes%d" % h, align_bytes=64) for h in range(2)]
@@ -77,15 +77,19 @@ def tile_attend_at_lse_topk_kernel(tc, qT, k_words, k_scales, vT, ls, us, offs, 
             values.tile([P, 2 * P], U8, name="q_scale%d" % h, align_bytes=64, offset=v_blocks * V_BYTES + 256 * h)
             for h in range(2)
         ]
-        for h in range(2):
-            nc.vector.quantize_mx(out=q_codes[h][:].bitcast(FP8X4), scales=q_scale[h][:], in_=q_bf[h][:])
+        nc.vector.quantize_mx(out=q_codes[0][:].bitcast(FP8X4), scales=q_scale[0][:], in_=q_bf[0][:])
         k_codes = []
         for s in range(2):
             picked_words = values.tile(
-                [P, N // 2], U32, name="k_codes%d" % s, align_bytes=64, offset=(v_blocks + 2) * V_BYTES + 1536 + 1024 * s
+                [P, N // 2], U32, name="k_codes%d" % s, align_bytes=64, offset=(v_blocks + 2) * V_BYTES + 1024 * s
             )
             nc.vector.tensor_copy(picked_words[:], k_word_pool[:].bitcast(U32).indirect(offsets[:, s * 16 : (s + 1) * 16]))
             k_codes.append(picked_words)
+        nc.vector.tensor_copy(second_pair, q_rows[1])
+        nc.vector.quantize_mx(out=q_codes[1][:].bitcast(FP8X4), scales=q_scale[1][:], in_=q_bf[1][:])
+
+        neg_ls = values.tile([P, q_tiles], F32, name="neg_ls", offset=(v_blocks + 2) * V_BYTES + 2048)
+        nc.vector.tensor_scalar(neg_ls[:], ls_sb[:], -1.0, 0.0, MULT, ADD)
 
         def scores(dest, j, s):
             cols = slice((j % 2) * P, (j % 2 + 1) * P)
@@ -99,21 +103,22 @@ def tile_attend_at_lse_topk_kernel(tc, qT, k_words, k_scales, vT, ls, us, offs, 
                 stop=True,
             )
 
-        def exponentials(dest, source, j):
+        def exponentials(dest, source, bias):
             source = source.rearrange("m (p t) -> m t p", t=PACK)
-            nc.scalar.activation(dest, source, EXP, bias=neg_ls[:, j : j + 1], scale=1.0)
+            nc.scalar.activation(dest, source, EXP, bias=bias, scale=1.0)
 
         expd = [keep.tile([P, PACK, P], F32, name="expd%d" % j) for j in range(q_tiles)]
         for s in range(2):
             for j in range(2):
                 sums = bank(2 * s + j, [P, N // 2], "scores%d_%d" % (j, s))
                 scores(sums[:], j, s)
-                exponentials(expd[j][:, :, s * P // 2 : (s + 1) * P // 2], sums[:], j)
-        for j in range(2, q_tiles):
-            sums = bank(3 + j, [P, N], "scores%d" % j)
+                exponentials(expd[j][:, :, s * P // 2 : (s + 1) * P // 2], sums[:], (neg_ls_first, neg_ls)[s][:, j : j + 1])
+
+        def whole_tile(j, number):
+            sums = bank(number, [P, N], "scores%d" % j)
             for s in range(2):
                 scores(sums[:, s * N // 2 : (s + 1) * N // 2], j, s)
-            exponentials(expd[j][:], sums[:], j)
+            exponentials(expd[j][:], sums[:], neg_ls[:, j : j + 1])
 
         y_bf = [values.tile([P, 2 * N], BF16, name="y_bf%d" % h, align_bytes=64, offset=2048 * h) for h in range(2)]
         y_codes = [keep.tile([P, 2 * P], U32, name="y_codes%d" % h, align_bytes=64) for h in range(2)]
@@ -139,22 +144,17 @@ def tile_attend_at_lse_topk_kernel(tc, qT, k_words, k_scales, vT, ls, us, offs, 
                 nc.scalar.activation(picked[:, 16 * cut :], v_pool[c][:].indirect(offsets[:, cut:]), COPY)
             return picked
 
-        def turn_values(c, picked):
+        def turn_values(c, picked, v_bf):
             words = picked[:].bitcast(F32)
             turned = bank((2, 3, 5, 6)[c], [P, 2, P], "v_turned%d" % c)
             for u in range(2):
                 nc.tensor.transpose(turned[:, u, :], words[:, u : N // 2 : 2], ident[:])
-            if c in (0, 2):
-                v_bf = values.tile([P, N], BF16, name="v_bf%d" % c, align_bytes=64, offset=(c + 1) * V_BYTES + 1024)
-            else:
-                v_bf = keep.tile([P, N], BF16, name="v_bf%d" % c, align_bytes=64)
-            nc.scalar.copy(v_bf[:].bitcast(F32).rearrange("p (e u) -> p e u", u=2), turned[:].rearrange("p u e -> p e u"))
-            return v_bf
+            nc.scalar.copy(v_bf.bitcast(F32).rearrange("p (e u) -> p e u", u=2), turned[:].rearrange("p u e -> p e u"))
 
-        def quantize_values(c, v_bf):
-            nc.vector.quantize_mx(out=v_codes[c][:].bitcast(FP8X4), scales=v_scale[c][:], in_=v_bf[:])
+        def quantize_values(codes, scale, v_bf):
+            nc.vector.quantize_mx(out=codes.bitcast(FP8X4), scales=scale, in_=v_bf)
 
-        out_rows = out[0].rearrange("(m j) e -> m j e", j=q_tiles)
+        out_rows = out[0].rearrange("(h m i) e -> h m i e", h=2, i=2)
 
         def multiply(dest, j, codes, scale):
             cols = slice((j % 2) * P, (j % 2 + 1) * P)
@@ -168,47 +168,62 @@ def tile_attend_at_lse_topk_kernel(tc, qT, k_words, k_scales, vT, ls, us, offs, 
                 stop=True,
             )
 
-        def product(c, banks, copies, offset):
-            tiles_a_bank = q_tiles // len(banks)
-            for h, number in enumerate(banks):
-                sums = bank(number, [P, tiles_a_bank, P], "product%d_%d" % (c, h))
-                first = h * tiles_a_bank
-                for i in range(tiles_a_bank):
-                    multiply(sums[:, i, :], first + i, v_codes[c][:], v_scale[c][:])
-                result = values.tile([P, tiles_a_bank, P], F32, name="result%d_%d" % (c, h), offset=offset + 1024 * h)
-                copies[h](result[:], sums[:])
-                nc.sync.dma_start(out_rows[:, first : first + tiles_a_bank, c * P : (c + 1) * P], result[:])
+        def product(c, h, number):
+            sums = bank(number, [P, 2, P], "product%d_%d" % (c, h))
+            for i in range(2):
+                multiply(sums[:, i, :], 2 * h + i, codes[c][:], scale[c][:])
+            return sums
 
-        v_codes = [
-            keep.tile([P, P], U32, name="v_codes0", align_bytes=64),
-            values.tile([P, P], U32, name="v_codes1", align_bytes=64, offset=2 * V_BYTES),
-            values.tile([P, P], U32, name="v_codes2", align_bytes=64, offset=3 * V_BYTES),
-            keep.tile([P, P], U32, name="v_codes3", align_bytes=64),
-        ]
-        v_scale = [keep.tile([P, P], U8, name="v_scale%d" % c, align_bytes=64) for c in range(v_blocks)]
+        def store(c, h, sums, copy, offset):
+            result = values.tile([P, 2, P], F32, name="result%d_%d" % (c, h), offset=offset)
+            copy(result[:], sums[:])
+            nc.sync.dma_start(out_rows[h, :, :, c * P : (c + 1) * P], result[:])
 
         picked = gather_values(0)
-        for j in range(q_tiles):
+        whole_tile(2, 5)
+        weights(0)
+        whole_tile(3, 6)
+        for j in range(1, q_tiles):
             weights(j)
         picked1 = gather_values(1)
-        v_bf0 = turn_values(0, picked)
+        v_bf = [
+            values.tile([P, N], BF16, name="v_bf0", align_bytes=64, offset=V_BYTES),
+            keep.tile([P, N], BF16, name="v_bf1", align_bytes=64),
+            values.tile([P, N], BF16, name="v_bf2", align_bytes=64, offset=3 * V_BYTES),
+            values.tile([P, N], BF16, name="v_bf3", align_bytes=64, offset=5120),
+        ]
+        codes = [
+            keep.tile([P, P], U32, name="v_codes0", align_bytes=64),
+            values.tile([P, P], U32, name="v_codes1", align_bytes=64, offset=2 * V_BYTES),
+            keep.tile([P, P], U32, name="v_codes2", align_bytes=64),
+            keep.tile([P, P], U32, name="v_codes3", align_bytes=64),
+        ]
+        scale = [keep.tile([P, P], U8, name="v_scale%d" % c, align_bytes=64) for c in range(v_blocks)]
+        turn_values(0, picked, v_bf[0][:])
         quantize_weights(0)
         quantize_weights(1)
-        quantize_values(0, v_bf0)
-        v_bf1 = turn_values(1, picked1)
+        quantize_values(codes[0][:], scale[0][:], v_bf[0][:])
+        turn_values(1, picked1, v_bf[1][:])
         picked2 = gather_values(2)
-        quantize_values(1, v_bf1)
-        product(0, (4,), (nc.vector.tensor_copy,), 2 * V_BYTES + 2048)
-        v_bf2 = turn_values(2, picked2)
+        quantize_values(codes[1][:], scale[1][:], v_bf[1][:])
+        store(0, 0, product(0, 0, 4), nc.scalar.copy, 2 * V_BYTES + 1024)
         picked3 = gather_values(3)
-        quantize_values(2, v_bf2)
-        product(1, (7,), (nc.vector.tensor_copy,), 3 * V_BYTES + 2048)
-        v_bf3 = turn_values(3, picked3)
-        quantize_values(3, v_bf3)
-        product(2, (0, 1), (nc.vector.tensor_copy, nc.scalar.copy), 4096)
+        turn_values(2, picked2, v_bf[2][:])
+        store(1, 0, product(1, 0, 7), nc.vector.tensor_copy, 3 * V_BYTES + 1024)
+        quantize_values(codes[2][:], scale[2][:], v_bf[2][:])
+        store(1, 1, product(1, 1, 0), nc.scalar.copy, 3 * V_BYTES + 2048)
+        store(0, 1, product(0, 1, 4), nc.vector.tensor_copy, 3 * V_BYTES)
+        warm = bank(1, [P, 3, P], "warm")
+        for j in range(3):
+            multiply(warm[:, j, :], j, codes[1][:], scale[1][:])
+        turn_values(3, picked3, v_bf[3][:])
+        quantize_values(codes[3][:], scale[3][:], v_bf[3][:])
+        store(2, 0, product(2, 0, 2), nc.scalar.copy, 4096)
+        store(2, 1, product(2, 1, 3), nc.vector.tensor_copy, 5120)
+        codes3, scale3 = codes[3], scale[3]
         last = keep.tile([P, q_tiles, P], F32, name="last")
         for j in range(q_tiles):
-            sums = bank((2, 3, 4, 5)[j], [P, P], "last_product%d" % j)
-            multiply(sums[:], j, v_codes[3][:], v_scale[3][:])
+            sums = bank((5, 1, 7, 0)[j], [P, P], "last_product%d" % j)
+            multiply(sums[:], j, codes3[:], scale3[:])
             (nc.scalar.copy, nc.vector.tensor_copy)[j % 2](last[:, j, :], sums[:])
-            (nc.scalar, nc.sync)[j % 2].dma_start(out_rows[:, j, 3 * P :], last[:, j, :])
+            (nc.scalar, nc.sync)[j % 2].dma_start(out_rows[j // 2, :, j % 2, 3 * P :], last[:, j, :])

@@ -213,9 +213,6 @@ def tile_attend_at_lse_topk_kernel(tc, qT, k_words, k_scales, vT, ls, us, offs, 
         quantize_values(codes[2][:], scale[2][:], v_bf[2][:])
         store(1, 1, product(1, 1, 0), nc.scalar.copy, 3 * V_BYTES + 2048)
         store(0, 1, product(0, 1, 4), nc.vector.tensor_copy, 3 * V_BYTES)
-        warm = bank(1, [P, 3, P], "warm")
-        for j in range(3):
-            multiply(warm[:, j, :], j, codes[1][:], scale[1][:])
         turn_values(3, picked3, v_bf[3][:])
         quantize_values(codes[3][:], scale[3][:], v_bf[3][:])
         store(2, 0, product(2, 0, 2), nc.scalar.copy, 4096)

@@ -215,12 +215,18 @@ def tile_attend_at_lse_topk_kernel(tc, qT, k_words, k_scales, vT, ls, us, offs, 
         store(0, 1, product(0, 1, 4), nc.vector.tensor_copy, 3 * V_BYTES)
         turn_values(3, picked3, v_bf[3][:])
         quantize_values(codes[3][:], scale[3][:], v_bf[3][:])
-        store(2, 0, product(2, 0, 2), nc.scalar.copy, 4096)
-        store(2, 1, product(2, 1, 3), nc.vector.tensor_copy, 5120)
+        for h in range(2):
+            result = values.tile([P, 2, P], F32, name="result2_%d" % h, offset=4096 + 1024 * h)
+            for i in range(2):
+                j = 2 * h + i
+                sums = bank((2, 3, 1, 5)[j], [P, P], "product2_%d" % j)
+                multiply(sums[:], j, codes[2][:], scale[2][:])
+                (nc.vector.tensor_copy if j == 3 else nc.scalar.copy)(result[:, i, :], sums[:])
+            nc.sync.dma_start(out_rows[h, :, :, 2 * P : 3 * P], result[:])
         codes3, scale3 = codes[3], scale[3]
         last = keep.tile([P, q_tiles, P], F32, name="last")
         for j in range(q_tiles):
-            sums = bank((5, 1, 7, 0)[j], [P, P], "last_product%d" % j)
+            sums = bank((6, 4, 7, 0)[j], [P, P], "last_product%d" % j)
             multiply(sums[:], j, codes3[:], scale3[:])
             (nc.scalar.copy, nc.vector.tensor_copy)[j % 2](last[:, j, :], sums[:])
             (nc.scalar, nc.sync)[j % 2].dma_start(out_rows[j // 2, :, j % 2, 3 * P :], last[:, j, :])

@@ -207,12 +207,12 @@ def tile_attend_at_lse_topk_kernel(tc, qT, k_words, k_scales, vT, ls, us, offs, 
         picked2 = gather_values(2)
         quantize_values(codes[1][:], scale[1][:], v_bf[1][:])
         store(0, 0, product(0, 0, 4), nc.scalar.copy, 2 * V_BYTES + 1024)
+        store(0, 1, product(0, 1, 1), nc.vector.tensor_copy, 2 * V_BYTES + 2048)
         picked3 = gather_values(3)
         turn_values(2, picked2, v_bf[2][:])
         store(1, 0, product(1, 0, 7), nc.vector.tensor_copy, 3 * V_BYTES + 1024)
         quantize_values(codes[2][:], scale[2][:], v_bf[2][:])
         store(1, 1, product(1, 1, 0), nc.scalar.copy, 3 * V_BYTES + 2048)
-        store(0, 1, product(0, 1, 4), nc.vector.tensor_copy, 3 * V_BYTES)
         turn_values(3, picked3, v_bf[3][:])
         quantize_values(codes[3][:], scale[3][:], v_bf[3][:])
         for h in range(2):

from contextlib import ExitStack

import concourse.mybir as mybir
from concourse.masks import make_identity

F32 = mybir.dt.float32
BF16 = mybir.dt.bfloat16
I32 = mybir.dt.int32
U32 = mybir.dt.uint32
U16 = mybir.dt.uint16
U8 = mybir.dt.uint8
FP8X4 = mybir.dt.float8_e4m3fn_x4
MULT = mybir.AluOpType.mult
ADD = mybir.AluOpType.add
COPY = mybir.ActivationFunctionType.Copy
EXP = mybir.ActivationFunctionType.Exp

P = 128
PACK = 4
T, N, D, NQ, DV = 2048, 512, 512, 512, 512
V_BYTES = T * 4
LIST_COLS = N // 16
FLOPS = 2 * D * N * NQ + 2 * N * NQ * DV
ON_VECTOR = (32, 0, 16, 16)


def tile_attend_at_lse_topk_kernel(tc, qT, k_words, k_scales, vT, ls, us, offs, out):
    nc = tc.nc
    q_tiles = NQ // P
    v_blocks = DV // P
    with ExitStack() as ctx:
        keep = ctx.enter_context(tc.tile_pool(name="keep", bufs=1))
        values = ctx.enter_context(tc.tile_pool(name="values", bufs=1))
        psum = ctx.enter_context(tc.psum_pool(name="psum", bufs=1))

        def bank(number, shape, name):
            return psum.tile(shape, F32, name=name, tag="bank%d" % number)

        q_halves = qT[0].rearrange("(p r) (h q) -> h p r q", r=PACK, h=2)
        q_raw = [keep.tile([P, PACK, NQ // 2], F32, name="q_raw%d" % h) for h in range(2)]
        nc.sync.dma_start(q_raw[0][:], q_halves[0])
        offsets = keep.tile([P, LIST_COLS], U16, name="offsets")
        nc.sync.dma_start(offsets[:], offs)
        ls_sb = keep.tile([P, q_tiles], F32, name="ls_sb")
        nc.sync.dma_start(ls_sb[:].rearrange("m (h i) -> m h i", h=2), ls[0, 0].rearrange("(h m i) -> m h i", h=2, i=2))
        k_scale_pool = values.tile([P, T], U8, name="k_scale_pool", offset=v_blocks * V_BYTES)
        nc.vector.memset(k_scale_pool[:].bitcast(I32), 0)
        for r in range(4):
            nc.sync.dma_start(k_scale_pool[r:P:32, :].bitcast(I32), k_scales[0, r:16:4, :].bitcast(I32))
        k_word_pool = values.tile([P, T], I32, name="k_word_pool", offset=(v_blocks + 1) * V_BYTES)
        nc.sync.dma_start(k_word_pool[:], k_words[0].rearrange("p t r -> p (t r)").bitcast(I32))
        nc.sync.dma_start(q_raw[1][:], q_halves[1])
        us_sb = keep.tile([P, PACK], F32, name="us_sb")
        nc.sync.dma_start(us_sb[:], us[0].rearrange("(p t) o -> p (t o)", t=PACK))
        v_pool = []
        for c in range(v_blocks):
            block = values.tile([P, T], F32, name="v_pool%d" % c, offset=c * V_BYTES)
            nc.sync.dma_start(block[:], vT[c * P : (c + 1) * P, :])
            v_pool.append(block)

        ident = keep.tile([P, P], F32, name="ident")
        make_identity(nc, ident[:])
        neg_ls_first = keep.tile([P, 2], F32, name="neg_ls_first")

        q_rows = [half[:].rearrange("p r (m i) -> p m r i", i=2) for half in q_raw]
        q_bf = [
            values.tile([P, 2 * N], BF16, name="q_bf%d" % h, align_bytes=64, offset=(v_blocks + 2) * V_BYTES + 2048 * h)
            for h in range(2)
        ]
        nc.scalar.copy(q_bf[0][:].rearrange("p (j m r) -> p m r j", j=2, r=PACK), q_rows[0])
        second_pair = q_bf[1][:].rearrange("p (j m r) -> p m r j", j=2, r=PACK)
        nc.gpsimd.tensor_scalar(neg_ls_first[:], ls_sb[:, 0:2], -1.0, 0.0, MULT, ADD)
        k_scale = keep.tile([P, N], U8, name="k_scale", align_bytes=64)
        nc.vector.tensor_copy(k_scale[:], k_scale_pool[:].indirect(offsets[:]))
        q_codes = [keep.tile([P, 2 * P], U32, name="q_codes%d" % h, align_bytes=64) for h in range(2)]
        q_scale = [
            values.tile([P, 2 * P], U8, name="q_scale%d" % h, align_bytes=64, offset=v_blocks * V_BYTES + 256 * h)
            for h in range(2)
        ]
        nc.vector.quantize_mx(out=q_codes[0][:].bitcast(FP8X4), scales=q_scale[0][:], in_=q_bf[0][:])
        k_codes = []
        for s in range(2):
            picked_words = values.tile(
                [P, N // 2], U32, name="k_codes%d" % s, align_bytes=64, offset=(v_blocks + 2) * V_BYTES + 1024 * s
            )
            nc.vector.tensor_copy(picked_words[:], k_word_pool[:].bitcast(U32).indirect(offsets[:, s * 16 : (s + 1) * 16]))
            k_codes.append(picked_words)
        nc.vector.tensor_copy(second_pair, q_rows[1])
        nc.vector.quantize_mx(out=q_codes[1][:].bitcast(FP8X4), scales=q_scale[1][:], in_=q_bf[1][:])

        neg_ls = values.tile([P, q_tiles], F32, name="neg_ls", offset=(v_blocks + 2) * V_BYTES + 2048)
        nc.vector.tensor_scalar(neg_ls[:], ls_sb[:], -1.0, 0.0, MULT, ADD)

        def scores(dest, j, s):
            cols = slice((j % 2) * P, (j % 2 + 1) * P)
            nc.tensor.matmul_mx(
                out=dest,
                lhsT=q_codes[j // 2][:, cols].bitcast(FP8X4),
                lhsT_scale=q_scale[j // 2][:, cols],
                rhs=k_codes[s][:].bitcast(FP8X4),
                rhs_scale=k_scale[:, s * N // 2 : (s + 1) * N // 2],
                start=True,
                stop=True,
            )

        def exponentials(dest, source, bias):
            source = source.rearrange("m (p t) -> m t p", t=PACK)
            nc.scalar.activation(dest, source, EXP, bias=bias, scale=1.0)

        expd = [keep.tile([P, PACK, P], F32, name="expd%d" % j) for j in range(q_tiles)]
        for s in range(2):
            for j in range(2):
                sums = bank(2 * s + j, [P, N // 2], "scores%d_%d" % (j, s))
                scores(sums[:], j, s)
                exponentials(expd[j][:, :, s * P // 2 : (s + 1) * P // 2], sums[:], (neg_ls_first, neg_ls)[s][:, j : j + 1])

        def whole_tile(j, number):
            sums = bank(number, [P, N], "scores%d" % j)
            for s in range(2):
                scores(sums[:, s * N // 2 : (s + 1) * N // 2], j, s)
            exponentials(expd[j][:], sums[:], neg_ls[:, j : j + 1])

        y_bf = [values.tile([P, 2 * N], BF16, name="y_bf%d" % h, align_bytes=64, offset=2048 * h) for h in range(2)]
        y_codes = [keep.tile([P, 2 * P], U32, name="y_codes%d" % h, align_bytes=64) for h in range(2)]
        y_scale = [keep.tile([P, 2 * P], U8, name="y_scale%d" % h, align_bytes=64) for h in range(2)]
        us_spread = us_sb[:].unsqueeze(1).to_broadcast([P, P, PACK])

        def weights(j):
            turned = bank((4, 7, 0, 1)[j], [P, PACK, P], "y_turned%d" % j)
            for t in range(PACK):
                nc.tensor.transpose(turned[:, t, :], expd[j][:, t, :], ident[:])
            dest = y_bf[j // 2][:, (j % 2) * N : (j % 2 + 1) * N].rearrange("p (m t) -> p m t", t=PACK)
            nc.vector.tensor_tensor(dest, turned[:].rearrange("p t m -> p m t"), us_spread, MULT)

        def quantize_weights(h):
            nc.vector.quantize_mx(out=y_codes[h][:].bitcast(FP8X4), scales=y_scale[h][:], in_=y_bf[h][:])

        def gather_values(c):
            picked = keep.tile([P, N], BF16, name="v_picked%d" % c)
            cut = ON_VECTOR[c]
            if cut > 0:
                nc.vector.tensor_copy(picked[:, : 16 * cut], v_pool[c][:].indirect(offsets[:, :cut]))
            if cut < LIST_COLS:
                nc.scalar.activation(picked[:, 16 * cut :], v_pool[c][:].indirect(offsets[:, cut:]), COPY)
            return picked

        def turn_values(c, picked, v_bf):
            words = picked[:].bitcast(F32)
            turned = bank((2, 3, 5, 6)[c], [P, 2, P], "v_turned%d" % c)
            for u in range(2):
                nc.tensor.transpose(turned[:, u, :], words[:, u : N // 2 : 2], ident[:])
            nc.scalar.copy(v_bf.bitcast(F32).rearrange("p (e u) -> p e u", u=2), turned[:].rearrange("p u e -> p e u"))

        def quantize_values(codes, scale, v_bf):
            nc.vector.quantize_mx(out=codes.bitcast(FP8X4), scales=scale, in_=v_bf)

        out_rows = out[0].rearrange("(h m i) e -> h m i e", h=2, i=2)

        def multiply(dest, j, codes, scale):
            cols = slice((j % 2) * P, (j % 2 + 1) * P)
            nc.tensor.matmul_mx(
                out=dest,
                lhsT=y_codes[j // 2][:, cols].bitcast(FP8X4),
                lhsT_scale=y_scale[j // 2][:, cols],
                rhs=codes.bitcast(FP8X4),
                rhs_scale=scale,
                start=True,
                stop=True,
            )

        def product(c, h, number):
            sums = bank(number, [P, 2, P], "product%d_%d" % (c, h))
            for i in range(2):
                multiply(sums[:, i, :], 2 * h + i, codes[c][:], scale[c][:])
            return sums

        def store(c, h, sums, copy, offset):
            result = values.tile([P, 2, P], F32, name="result%d_%d" % (c, h), offset=offset)
            copy(result[:], sums[:])
            nc.sync.dma_start(out_rows[h, :, :, c * P : (c + 1) * P], result[:])

        picked = gather_values(0)
        whole_tile(2, 5)
        weights(0)
        whole_tile(3, 6)
        for j in range(1, q_tiles):
            weights(j)
        picked1 = gather_values(1)
        v_bf = [
            values.tile([P, N], BF16, name="v_bf0", align_bytes=64, offset=V_BYTES),
            keep.tile([P, N], BF16, name="v_bf1", align_bytes=64),
            values.tile([P, N], BF16, name="v_bf2", align_bytes=64, offset=3 * V_BYTES),
            values.tile([P, N], BF16, name="v_bf3", align_bytes=64, offset=5120),
        ]
        codes = [
            keep.tile([P, P], U32, name="v_codes0", align_bytes=64),
            values.tile([P, P], U32, name="v_codes1", align_bytes=64, offset=2 * V_BYTES),
            keep.tile([P, P], U32, name="v_codes2", align_bytes=64),
            keep.tile([P, P], U32, name="v_codes3", align_bytes=64),
        ]
        scale = [keep.tile([P, P], U8, name="v_scale%d" % c, align_bytes=64) for c in range(v_blocks)]
        turn_values(0, picked, v_bf[0][:])
        quantize_weights(0)
        quantize_weights(1)
        quantize_values(codes[0][:], scale[0][:], v_bf[0][:])
        turn_values(1, picked1, v_bf[1][:])
        picked2 = gather_values(2)
        quantize_values(codes[1][:], scale[1][:], v_bf[1][:])
        store(0, 0, product(0, 0, 4), nc.scalar.copy, 2 * V_BYTES + 1024)
        store(0, 1, product(0, 1, 1), nc.vector.tensor_copy, 2 * V_BYTES + 2048)
        picked3 = gather_values(3)
        turn_values(2, picked2, v_bf[2][:])
        store(1, 0, product(1, 0, 7), nc.vector.tensor_copy, 3 * V_BYTES + 1024)
        quantize_values(codes[2][:], scale[2][:], v_bf[2][:])
        store(1, 1, product(1, 1, 0), nc.scalar.copy, 3 * V_BYTES + 2048)
        turn_values(3, picked3, v_bf[3][:])
        quantize_values(codes[3][:], scale[3][:], v_bf[3][:])
        for h in range(2):
            result = values.tile([P, 2, P], F32, name="result2_%d" % h, offset=4096 + 1024 * h)
            for i in range(2):
                j = 2 * h + i
                sums = bank((2, 3, 1, 5)[j], [P, P], "product2_%d" % j)
                multiply(sums[:], j, codes[2][:], scale[2][:])
                (nc.vector.tensor_copy if j == 3 else nc.scalar.copy)(result[:, i, :], sums[:])
            nc.sync.dma_start(out_rows[h, :, :, 2 * P : 3 * P], result[:])
        codes3, scale3 = codes[3], scale[3]
        last = keep.tile([P, q_tiles, P], F32, name="last")
        for j in range(q_tiles):
            sums = bank((6, 4, 7, 0)[j], [P, P], "last_product%d" % j)
            multiply(sums[:], j, codes3[:], scale3[:])
            (nc.scalar.copy, nc.vector.tensor_copy)[j % 2](last[:, j, :], sums[:])
            (nc.scalar, nc.sync)[j % 2].dma_start(out_rows[j // 2, :, j % 2, 3 * P :], last[:, j, :])
